import numpy as np
import ml_dtypes


def mxq(x, axis, fmt="e4m3"):
    dtype, down = {"e4m3": (ml_dtypes.float8_e4m3fn, 7), "e5m2": (ml_dtypes.float8_e5m2, 14)}[fmt]
    v = np.moveaxis(np.asarray(x, np.float32).astype(ml_dtypes.bfloat16).astype(np.float64), axis, -1)
    blocks = v.reshape(v.shape[:-1] + (-1, 32))
    amax = np.abs(blocks).max(-1, keepdims=True)
    byte = np.maximum(np.where(amax > 0, np.frexp(amax)[1] - 1 + 127, 0) - down, 1)
    scale = np.exp2(byte - 127.0)
    codes = (blocks / scale).astype(np.float32).astype(dtype).astype(np.float64)
    return np.moveaxis((codes * scale).reshape(v.shape), -1, axis)


WIDE = False


def mx_kscale(k):
    if not WIDE:
        return np.ones(k)
    levels = np.array([10, -10, 5, -5, 0])
    if k % 512:
        return np.exp2(np.random.permutation(np.resize(levels, k // 32))).repeat(32)
    a = np.empty((k // 512, 16))
    for p in range(k // 512):
        a[p, :8] = np.random.permutation(np.resize(levels, 8))
        for g in range(8):
            far = levels[np.abs(levels - a[p, g]) >= 10]
            a[p, g + 8] = far[np.random.randint(len(far))]
    return np.exp2(a.ravel()).repeat(32)


def f64(x):
    return np.asarray(x).astype(np.float64)


def striped(idx):
    return np.tile(np.asarray(idx).reshape(-1, 16).T, (8, 1)).astype(np.uint16)


def unstriped(offs):
    return offs[:16].T.reshape(-1).astype(np.int64)


E2M1 = np.array([0.0, 0.5, 1.0, 1.5, 2.0, 3.0, 4.0, 6.0, -0.0, -0.5, -1.0, -1.5, -2.0, -3.0, -4.0, -6.0])


def pack_weight(w, fmt):
    k, n = w.shape
    w = f64(np.asarray(w, np.float32).astype(ml_dtypes.bfloat16)).reshape(k // 32, 32, n)
    amax = np.abs(w).max(1)
    if fmt == "e4m3":
        byte = np.frexp(amax)[1] - 1 + 127 - 7
    else:
        mant, ex = np.frexp(amax / 6.0)
        byte = np.where(mant > 0.5, ex, ex - 1) + 127
    byte = np.clip(np.where(amax > 0, byte, 1), 1, 254)
    scaled = (w * np.exp2(127.0 - byte)[:, None, :]).reshape(k, n).astype(np.float32)
    by_word = np.ascontiguousarray(scaled.reshape(k // 512, 128, 4, n).transpose(0, 1, 3, 2))
    if fmt == "e4m3":
        words = by_word.astype(ml_dtypes.float8_e4m3fn).view(np.uint8)
    else:
        c = by_word.astype(ml_dtypes.float4_e2m1fn).view(np.uint8) & 0xF
        words = (c[..., 0::2] | (c[..., 1::2] << 4)).reshape(k // 512, 128, 2 * n)
    return np.ascontiguousarray(words), np.ascontiguousarray(byte.astype(np.uint8).reshape(k // 512, 16, n))


def unpack_weight(words, scales, fmt):
    g, _, n = scales.shape
    words = np.ascontiguousarray(words).reshape(g, 128, n, -1)
    if fmt == "e4m3":
        vals = words.view(ml_dtypes.float8_e4m3fn).astype(np.float64)
    else:
        nib = np.empty((g, 128, n, 4), np.uint8)
        nib[..., 0::2] = words & 0xF
        nib[..., 1::2] = words >> 4
        vals = E2M1[nib]
    vals = vals * np.repeat(np.exp2(scales.astype(np.float64) - 127.0), 8, axis=1)[..., None]
    return vals.transpose(0, 1, 3, 2).reshape(g * 512, n)


B, N, T, D, DV, NQ = 2, 1024, 4096, 512, 256, 128
PAGE = 512
CAP = 2.0


def setup_inputs():
    n = np.random.standard_normal
    pages = np.random.permutation(T // PAGE)[:B * N // PAGE]
    idx = (pages[:, None] * PAGE + np.arange(PAGE)[None, :]).reshape(-1)
    s = mx_kscale(D)[:, None]
    u = np.ones(T)
    u[idx] = mx_kscale(B * N)
    r = np.random.uniform(0.5, 2.0, T)
    k = n((D, T)) / s
    v = n((DV, T)) / (u * r)
    kp = pack_weight(k, "e4m3")
    vp = pack_weight(v.T, "e4m3")
    return {
        "qT": (n((B, D, NQ)) * s * (0.80 / np.sqrt(D))).astype(np.float32),
        "k_words": kp[0],
        "k_scales": kp[1],
        "v_words": vp[0],
        "v_scales": vp[1],
        "vs": np.tile(u * r, (128, 1)).astype(np.float32),
        "offs": striped(idx),
        "voffs": striped((pages[:, None] * DV + np.arange(DV)[None, :]).reshape(-1)),
    }


def reference(qT, k_words, k_scales, v_words, v_scales, vs, offs, voffs):
    idx = unstriped(offs)
    k = unpack_weight(k_words, k_scales, "e4m3")
    v = unpack_weight(v_words, v_scales, "e4m3")
    v = v.reshape(T // 512, 512, DV)[unstriped(voffs)[::DV] // DV].reshape(B, N, DV)
    pick = lambda x: x[:, idx].reshape(x.shape[0], B, N).transpose(1, 0, 2)
    q = f64(qT)
    score = mxq(q, 1, "e4m3").transpose(0, 2, 1) @ pick(k)
    score = CAP * np.tanh(score / CAP)
    p = 1.0 / (1.0 + np.exp(-score))
    w = p * pick(f64(vs))[:, :1, :]
    y = mxq(w, 2, "e4m3") @ v
    y = y / 16.0
    return y

@@ -1,0 +1,175 @@
+from contextlib import ExitStack
+
+import concourse.mybir as mybir
+from concourse.masks import make_identity
+
+F32 = mybir.dt.float32
+BF16 = mybir.dt.bfloat16
+I32 = mybir.dt.int32
+U32 = mybir.dt.uint32
+U16 = mybir.dt.uint16
+U8 = mybir.dt.uint8
+FP8X4 = mybir.dt.float8_e4m3fn_x4
+ACT = mybir.ActivationFunctionType
+ALU = mybir.AluOpType
+
+P = 128
+B, N, T, D, DV, NQ = 2, 1024, 4096, 512, 256, 128
+PAGE = 512
+PAGES = B * N // PAGE
+POOL_PAGES = T // PAGE
+V_ROW = 4
+
+FLOPS = 2 * B * NQ * N * (D + DV)
+BYTES = B * D * NQ * 4 + T * D + 16 * T + T * DV + 16 * POOL_PAGES * DV + T * 4 + P * (B * N + PAGES * DV) // 16 * 2 + B * NQ * DV * 4
+
+
+def tile_attend_pkv8_sigm_cap_kernel(tc, qT, k_words, k_scales, v_words, v_scales, vs, offs, voffs, out):
+    nc = tc.nc
+    with ExitStack() as ctx:
+        keep = ctx.enter_context(tc.tile_pool(name="keep", bufs=1))
+        turn = ctx.enter_context(tc.psum_pool(name="turn", bufs=3))
+        score = ctx.enter_context(tc.psum_pool(name="score", bufs=3))
+        acc = ctx.enter_context(tc.psum_pool(name="acc", bufs=2))
+
+        def sb(shape, dtype, name, tag=None):
+            return keep.tile(shape, dtype, name=name, tag=tag or name, align_bytes=64)
+
+        lst = keep.tile([P, B * N // 16], U16, name="lst")
+        vlst = keep.tile([P, PAGES * DV // 16], U16, name="vlst")
+        ks_pool = sb([P, T // 4], I32, "ks_pool")
+        vsc_pool = sb([P, POOL_PAGES * DV // 4], I32, "vsc_pool")
+        kw_pool = sb([P, T], I32, "kw_pool")
+        tok_row = sb([P, T // P], F32, "tok_row")
+        tok_pool = sb([P, T], F32, "tok_pool")
+        ident = sb([P, P], F32, "ident")
+
+        nc.vector.memset(ks_pool[:], 0)
+        make_identity(nc, ident[:])
+        nc.gpsimd.memset(vsc_pool[:], 0)
+        minus_two = sb([P, 1], F32, "minus_two")
+        nc.gpsimd.memset(minus_two[:], -2.0)
+
+        def load_queries(b):
+            raw = sb([P, 4, NQ], F32, "q_raw%d" % b, "q_raw")
+            nc.sync.dma_start(raw[:], qT[b].rearrange("(p j) q -> p j q", j=4))
+            return raw
+
+        nc.sync.dma_start(lst[:], offs)
+        nc.sync.dma_start(tok_row[:], vs[0:1, :].rearrange("o (p c) -> (o p) c", p=P))
+        nc.sync.dma_start(vlst[:], voffs)
+        q_raw = load_queries(0)
+        ks_rows = k_scales[0].bitcast(I32)
+        for g in range(4):
+            nc.scalar.dma_start(ks_pool[32 * g : 32 * g + 4, :], ks_rows[4 * g : 4 * g + 4, :])
+        nc.sync.dma_start(kw_pool[:], k_words[0].rearrange("p t r -> p (t r)").bitcast(I32))
+        vsc_rows = v_scales.bitcast(I32).rearrange("u f e -> f u e")
+        for g in range(4):
+            nc.gpsimd.dma_start(
+                vsc_pool[32 * g + V_ROW : 32 * g + V_ROW + 4, :].rearrange("f (u e) -> f u e", u=POOL_PAGES),
+                vsc_rows[4 * g : 4 * g + 4],
+            )
+
+        tok_view = tok_pool[:].rearrange("p (j c) -> p j c", c=T // P)
+        for a in range(T // PAGE):
+            bank = turn.tile([P, 4, P], F32, name="bank", tag="turn")
+            for cc in range(4):
+                c = 4 * a + cc
+                nc.tensor.transpose(bank[:, cc, :], tok_row[:, c : c + 1].to_broadcast([P, P]), ident[:])
+            nc.scalar.copy(tok_view[:, :, 4 * a : 4 * a + 4], bank[:].rearrange("p c j -> p j c"))
+
+        ks = [sb([P, N], U8, "ks%d" % b) for b in range(B)]
+        q_codes = [sb([P, NQ], U32, "q_codes%d" % b) for b in range(B)]
+        q_sc = [sb([P, NQ], U8, "q_sc%d" % b) for b in range(B)]
+
+        def gather_key_scales(b):
+            nc.vector.tensor_copy(ks[b][:], ks_pool[:].bitcast(U8).indirect(lst[:, b * 64 : (b + 1) * 64]))
+
+        def round_queries(b, raw, tag):
+            rounded = sb([P, NQ, 4], BF16, "q_bf%d" % b, tag)
+            nc.vector.tensor_copy(rounded[:], raw[:].rearrange("p j q -> p q j"))
+            return rounded
+
+        def quantise_queries(b, rounded):
+            nc.vector.quantize_mx(q_codes[b][:].bitcast(FP8X4), q_sc[b][:], rounded[:].rearrange("p q j -> p (q j)"))
+
+        gather_key_scales(0)
+        q_bf = round_queries(0, q_raw, "vw_pool")
+        q_raw = load_queries(1)
+        gather_key_scales(1)
+        quantise_queries(0, q_bf)
+        vw_pool = sb([P, POOL_PAGES * DV], I32, "vw_pool")
+        nc.sync.dma_start(
+            vw_pool[:].rearrange("p (u e) -> p u e", u=POOL_PAGES),
+            v_words.rearrange("u p e r -> p u (e r)").bitcast(I32),
+        )
+        vsc = sb([P, PAGES * DV], U8, "vsc")
+        nc.vector.tensor_copy(vsc[:], vsc_pool[:].bitcast(U8).indirect(vlst[:]))
+
+        kw = [sb([P, PAGE], U32, "kw%d" % e) for e in range(PAGES)]
+        prob = [sb([P, PAGE], F32, "prob%d" % e) for e in range(PAGES)]
+        for e in range(PAGES):
+            b, h = divmod(e, N // PAGE)
+            nc.vector.tensor_copy(kw[e][:], kw_pool[:].bitcast(U32).indirect(lst[:, e * 32 : (e + 1) * 32]))
+            if e == 1:
+                q_bf = round_queries(1, q_raw, "q_bf1")
+            if e == 2:
+                quantise_queries(1, q_bf)
+            sc = score.tile([P, PAGE], F32, name="sc")
+            nc.tensor.matmul_mx(
+                sc[:],
+                lhsT=q_codes[b][:].bitcast(FP8X4),
+                lhsT_scale=q_sc[b][:],
+                rhs=kw[e][:].bitcast(FP8X4),
+                rhs_scale=ks[b][:, h * PAGE : (h + 1) * PAGE],
+                start=True,
+                stop=True,
+            )
+            capped = sb([P, PAGE], F32, "capped%d" % e)
+            nc.scalar.activation(capped[:], sc[:], ACT.Sigmoid)
+            nc.scalar.activation(prob[e][:], capped[:], ACT.Sigmoid, scale=4.0, bias=minus_two[:])
+
+        vw = [sb([P, 2 * DV], U32, "vw%d" % b) for b in range(B)]
+        w_bf = [sb([P, NQ, 4], BF16, "w_bf%d" % e) for e in range(PAGES)]
+        y = [acc.tile([P, DV], F32, name="y%d" % b, tag="y") for b in range(B)]
+
+        def weigh(e):
+            w = sb([P, PAGE], F32, "w%d" % e)
+            nc.vector.tensor_tensor(w[:], tok_pool[:].indirect(lst[:, e * 32 : (e + 1) * 32]), prob[e][:], ALU.mult)
+            bank = turn.tile([P, 4, P], F32, name="bank", tag="turn")
+            for t in range(4):
+                nc.tensor.transpose(bank[:, t, :], w[:, t::4], ident[:])
+            nc.scalar.copy(w_bf[e][:], bank[:].rearrange("p t q -> p q t"))
+
+        def gather_values(b):
+            nc.vector.tensor_copy(vw[b][:], vw_pool[:].bitcast(U32).indirect(vlst[:, b * 32 : (b + 1) * 32]))
+
+        def mix(e):
+            b, h = divmod(e, N // PAGE)
+            w_codes = sb([P, NQ], U32, "w_codes%d" % e)
+            w_sc = sb([P, NQ], U8, "w_sc%d" % e)
+            nc.vector.quantize_mx(w_codes[:].bitcast(FP8X4), w_sc[:], w_bf[e][:].rearrange("p q t -> p (q t)"))
+            nc.tensor.matmul_mx(
+                y[b][:],
+                lhsT=w_codes[:].bitcast(FP8X4),
+                lhsT_scale=w_sc[:],
+                rhs=vw[b][:, h * DV : (h + 1) * DV].bitcast(FP8X4),
+                rhs_scale=vsc[V_ROW:P, e * DV : (e + 1) * DV],
+                start=(h == 0),
+                stop=(h == 1),
+            )
+            if h == 1:
+                res = sb([P, DV], F32, "res%d" % b)
+                nc.vector.tensor_scalar(res[:], y[b][:], 1.0 / 16.0, None, ALU.mult)
+                nc.sync.dma_start(out[b], res[:])
+
+        weigh(0)
+        gather_values(0)
+        weigh(1)
+        mix(0)
+        weigh(2)
+        mix(1)
+        weigh(3)
+        gather_values(1)
+        mix(2)
+        mix(3)

@@ -1,7 +1,6 @@
 from contextlib import ExitStack
 
 import concourse.mybir as mybir
-from concourse.masks import make_identity
 
 F32 = mybir.dt.float32
 BF16 = mybir.dt.bfloat16
@@ -38,88 +37,81 @@ def tile_attend_pkv8_sigm_cap_kernel(tc, qT, k_words, k_scales, v_words, v_scale
         lst = keep.tile([P, B * N // 16], U16, name="lst")
         vlst = keep.tile([P, PAGES * DV // 16], U16, name="vlst")
         ks_pool = sb([P, T // 4], I32, "ks_pool")
-        vsc_pool = sb([P, POOL_PAGES * DV // 4], I32, "vsc_pool")
-        kw_pool = sb([P, T], I32, "kw_pool")
-        tok_row = sb([P, T // P], F32, "tok_row")
-        tok_pool = sb([P, T], F32, "tok_pool")
         ident = sb([P, P], F32, "ident")
 
-        nc.vector.memset(ks_pool[:], 0)
-        make_identity(nc, ident[:])
-        nc.gpsimd.memset(vsc_pool[:], 0)
         minus_two = sb([P, 1], F32, "minus_two")
         nc.gpsimd.memset(minus_two[:], -2.0)
-
-        def load_queries(b):
-            raw = sb([P, 4, NQ], F32, "q_raw%d" % b, "q_raw")
-            nc.sync.dma_start(raw[:], qT[b].rearrange("(p j) q -> p j q", j=4))
-            return raw
-
-        nc.sync.dma_start(lst[:], offs)
-        nc.sync.dma_start(tok_row[:], vs[0:1, :].rearrange("o (p c) -> (o p) c", p=P))
-        nc.sync.dma_start(vlst[:], voffs)
-        q_raw = load_queries(0)
-        ks_rows = k_scales[0].bitcast(I32)
-        for g in range(4):
-            nc.scalar.dma_start(ks_pool[32 * g : 32 * g + 4, :], ks_rows[4 * g : 4 * g + 4, :])
-        nc.sync.dma_start(kw_pool[:], k_words[0].rearrange("p t r -> p (t r)").bitcast(I32))
-        vsc_rows = v_scales.bitcast(I32).rearrange("u f e -> f u e")
-        for g in range(4):
-            nc.gpsimd.dma_start(
-                vsc_pool[32 * g + V_ROW : 32 * g + V_ROW + 4, :].rearrange("f (u e) -> f u e", u=POOL_PAGES),
-                vsc_rows[4 * g : 4 * g + 4],
+        nc.vector.memset(ks_pool[:], 0)
+        half = P // 2
+        for h, tag in enumerate(("tok_pool", "kw_pool")):
+            zeros = sb([P, half], F32, "zeros%d" % h, tag)
+            nc.vector.memset(zeros[:], 0.0)
+            nc.gpsimd.affine_select(
+                out=ident[:, h * half : (h + 1) * half],
+                in_=zeros[:],
+                compare_op=ALU.not_equal,
+                fill=1.0,
+                base=-h * half,
+                pattern=[[-1, half]],
+                channel_multiplier=1,
             )
 
-        tok_view = tok_pool[:].rearrange("p (j c) -> p j c", c=T // P)
-        for a in range(T // PAGE):
-            bank = turn.tile([P, 4, P], F32, name="bank", tag="turn")
-            for cc in range(4):
-                c = 4 * a + cc
-                nc.tensor.transpose(bank[:, cc, :], tok_row[:, c : c + 1].to_broadcast([P, P]), ident[:])
-            nc.scalar.copy(tok_view[:, :, 4 * a : 4 * a + 4], bank[:].rearrange("p c j -> p j c"))
+        warm = sb([P, 1], F32, "warm")
+        nc.scalar.activation(warm[:], minus_two[:], ACT.Sigmoid)
+
+        nc.sync.dma_start(lst[:], offs)
+        nc.sync.dma_start(vlst[:], voffs)
+        ks_rows = k_scales[0].bitcast(I32)
+        for g in range(4):
+            nc.sync.dma_start(ks_pool[32 * g : 32 * g + 4, :], ks_rows[4 * g : 4 * g + 4, :])
+        q_raw = sb([P, B, 4, NQ], F32, "q_raw", "tok_pool")
+        nc.sync.dma_start(q_raw[:].rearrange("p b j q -> p b (j q)"), qT.rearrange("b (p j) q -> p b (j q)", j=4))
+        kw_pool = sb([P, T], I32, "kw_pool")
+        nc.sync.dma_start(kw_pool[:], k_words[0].rearrange("p t r -> p (t r)").bitcast(I32))
+
+        q_bf = [sb([P, NQ, 4], BF16, "q_bf%d" % b, ("vw_pool", "vsc_pool")[b]) for b in range(B)]
+        for b in range(B):
+            nc.scalar.copy(q_bf[b][:], q_raw[:, b].rearrange("p j q -> p q j"))
+        tok_pool = sb([P, T], F32, "tok_pool")
+        nc.sync.dma_start(tok_pool[:], vs)
 
         ks = [sb([P, N], U8, "ks%d" % b) for b in range(B)]
-        q_codes = [sb([P, NQ], U32, "q_codes%d" % b) for b in range(B)]
-        q_sc = [sb([P, NQ], U8, "q_sc%d" % b) for b in range(B)]
+        q_codes = sb([P, B * NQ], U32, "q_codes")
+        q_sc = sb([P, B * NQ], U8, "q_sc")
 
         def gather_key_scales(b):
             nc.vector.tensor_copy(ks[b][:], ks_pool[:].bitcast(U8).indirect(lst[:, b * 64 : (b + 1) * 64]))
 
-        def round_queries(b, raw, tag):
-            rounded = sb([P, NQ, 4], BF16, "q_bf%d" % b, tag)
-            nc.vector.tensor_copy(rounded[:], raw[:].rearrange("p j q -> p q j"))
-            return rounded
-
-        def quantise_queries(b, rounded):
-            nc.vector.quantize_mx(q_codes[b][:].bitcast(FP8X4), q_sc[b][:], rounded[:].rearrange("p q j -> p (q j)"))
-
         gather_key_scales(0)
-        q_bf = round_queries(0, q_raw, "vw_pool")
-        q_raw = load_queries(1)
         gather_key_scales(1)
-        quantise_queries(0, q_bf)
+        for b in range(B):
+            cols = slice(b * NQ, (b + 1) * NQ)
+            nc.vector.quantize_mx(q_codes[:, cols].bitcast(FP8X4), q_sc[:, cols], q_bf[b][:].rearrange("p q j -> p (q j)"))
         vw_pool = sb([P, POOL_PAGES * DV], I32, "vw_pool")
         nc.sync.dma_start(
             vw_pool[:].rearrange("p (u e) -> p u e", u=POOL_PAGES),
             v_words.rearrange("u p e r -> p u (e r)").bitcast(I32),
         )
-        vsc = sb([P, PAGES * DV], U8, "vsc")
-        nc.vector.tensor_copy(vsc[:], vsc_pool[:].bitcast(U8).indirect(vlst[:]))
+
+        vsc_pool = sb([P, POOL_PAGES * DV // 4], I32, "vsc_pool")
+        nc.gpsimd.memset(vsc_pool[:], 0)
+        vsc_rows = v_scales.bitcast(I32).rearrange("u f e -> f u e")
+        for g in range(4):
+            nc.sync.dma_start(
+                vsc_pool[32 * g + V_ROW : 32 * g + V_ROW + 4, :].rearrange("f (u e) -> f u e", u=POOL_PAGES),
+                vsc_rows[4 * g : 4 * g + 4],
+            )
 
         kw = [sb([P, PAGE], U32, "kw%d" % e) for e in range(PAGES)]
         prob = [sb([P, PAGE], F32, "prob%d" % e) for e in range(PAGES)]
         for e in range(PAGES):
             b, h = divmod(e, N // PAGE)
             nc.vector.tensor_copy(kw[e][:], kw_pool[:].bitcast(U32).indirect(lst[:, e * 32 : (e + 1) * 32]))
-            if e == 1:
-                q_bf = round_queries(1, q_raw, "q_bf1")
-            if e == 2:
-                quantise_queries(1, q_bf)
             sc = score.tile([P, PAGE], F32, name="sc")
             nc.tensor.matmul_mx(
                 sc[:],
-                lhsT=q_codes[b][:].bitcast(FP8X4),
-                lhsT_scale=q_sc[b][:],
+                lhsT=q_codes[:, b * NQ : (b + 1) * NQ].bitcast(FP8X4),
+                lhsT_scale=q_sc[:, b * NQ : (b + 1) * NQ],
                 rhs=kw[e][:].bitcast(FP8X4),
                 rhs_scale=ks[b][:, h * PAGE : (h + 1) * PAGE],
                 start=True,
@@ -129,8 +121,11 @@ def tile_attend_pkv8_sigm_cap_kernel(tc, qT, k_words, k_scales, v_words, v_scale
             nc.scalar.activation(capped[:], sc[:], ACT.Sigmoid)
             nc.scalar.activation(prob[e][:], capped[:], ACT.Sigmoid, scale=4.0, bias=minus_two[:])
 
-        vw = [sb([P, 2 * DV], U32, "vw%d" % b) for b in range(B)]
+        vsc = sb([P, PAGES * DV], U8, "vsc")
+        vw = [sb([P, DV], U32, "vw%d" % e) for e in range(PAGES)]
         w_bf = [sb([P, NQ, 4], BF16, "w_bf%d" % e) for e in range(PAGES)]
+        w_codes = [sb([P, NQ], U32, "w_codes%d" % e) for e in range(PAGES)]
+        w_sc = [sb([P, NQ], U8, "w_sc%d" % e) for e in range(PAGES)]
         y = [acc.tile([P, DV], F32, name="y%d" % b, tag="y") for b in range(B)]
 
         def weigh(e):
@@ -141,35 +136,32 @@ def tile_attend_pkv8_sigm_cap_kernel(tc, qT, k_words, k_scales, v_words, v_scale
                 nc.tensor.transpose(bank[:, t, :], w[:, t::4], ident[:])
             nc.scalar.copy(w_bf[e][:], bank[:].rearrange("p t q -> p q t"))
 
-        def gather_values(b):
-            nc.vector.tensor_copy(vw[b][:], vw_pool[:].bitcast(U32).indirect(vlst[:, b * 32 : (b + 1) * 32]))
+        def gather_values(e):
+            nc.vector.tensor_copy(vw[e][:], vw_pool[:].bitcast(U32).indirect(vlst[:, e * 16 : (e + 1) * 16]))
+
+        def quantise_weights(e):
+            nc.vector.quantize_mx(w_codes[e][:].bitcast(FP8X4), w_sc[e][:], w_bf[e][:].rearrange("p q t -> p (q t)"))
 
         def mix(e):
             b, h = divmod(e, N // PAGE)
-            w_codes = sb([P, NQ], U32, "w_codes%d" % e)
-            w_sc = sb([P, NQ], U8, "w_sc%d" % e)
-            nc.vector.quantize_mx(w_codes[:].bitcast(FP8X4), w_sc[:], w_bf[e][:].rearrange("p q t -> p (q t)"))
             nc.tensor.matmul_mx(
                 y[b][:],
-                lhsT=w_codes[:].bitcast(FP8X4),
-                lhsT_scale=w_sc[:],
-                rhs=vw[b][:, h * DV : (h + 1) * DV].bitcast(FP8X4),
+                lhsT=w_codes[e][:].bitcast(FP8X4),
+                lhsT_scale=w_sc[e][:],
+                rhs=vw[e][:].bitcast(FP8X4),
                 rhs_scale=vsc[V_ROW:P, e * DV : (e + 1) * DV],
                 start=(h == 0),
                 stop=(h == 1),
             )
             if h == 1:
                 res = sb([P, DV], F32, "res%d" % b)
-                nc.vector.tensor_scalar(res[:], y[b][:], 1.0 / 16.0, None, ALU.mult)
+                nc.scalar.activation(res[:], y[b][:], ACT.Copy, scale=1.0 / 16.0)
                 nc.sync.dma_start(out[b], res[:])
 
-        weigh(0)
-        gather_values(0)
-        weigh(1)
-        mix(0)
-        weigh(2)
-        mix(1)
-        weigh(3)
-        gather_values(1)
-        mix(2)
-        mix(3)
+        for e in range(PAGES):
+            weigh(e)
+        nc.vector.tensor_copy(vsc[:], vsc_pool[:].bitcast(U8).indirect(vlst[:]))
+        for e in range(PAGES):
+            quantise_weights(e)
+            gather_values(e)
+            mix(e)

@@ -1,6 +1,7 @@
 from contextlib import ExitStack
 
 import concourse.mybir as mybir
+from concourse.masks import make_identity
 
 F32 = mybir.dt.float32
 BF16 = mybir.dt.bfloat16
@@ -37,30 +38,28 @@ def tile_attend_pkv8_sigm_cap_kernel(tc, qT, k_words, k_scales, v_words, v_scale
         lst = keep.tile([P, B * N // 16], U16, name="lst")
         vlst = keep.tile([P, PAGES * DV // 16], U16, name="vlst")
         ks_pool = sb([P, T // 4], I32, "ks_pool")
+        vsc_pool = sb([P, POOL_PAGES * DV // 4], I32, "vsc_pool")
         ident = sb([P, P], F32, "ident")
 
+        one = sb([P, 1], F32, "one", "kw_pool")
         minus_two = sb([P, 1], F32, "minus_two")
-        nc.gpsimd.memset(minus_two[:], -2.0)
+        make_identity(nc, ident[:])
+        nc.vector.memset(vsc_pool[:], 0)
+        nc.vector.memset(one[:], 1.0)
         nc.vector.memset(ks_pool[:], 0)
-        half = P // 2
-        for h, tag in enumerate(("tok_pool", "kw_pool")):
-            zeros = sb([P, half], F32, "zeros%d" % h, tag)
-            nc.vector.memset(zeros[:], 0.0)
-            nc.gpsimd.affine_select(
-                out=ident[:, h * half : (h + 1) * half],
-                in_=zeros[:],
-                compare_op=ALU.not_equal,
-                fill=1.0,
-                base=-h * half,
-                pattern=[[-1, half]],
-                channel_multiplier=1,
-            )
+        nc.vector.tensor_scalar(minus_two[:], one[:], -2.0, None, ALU.mult)
 
         warm = sb([P, 1], F32, "warm")
         nc.scalar.activation(warm[:], minus_two[:], ACT.Sigmoid)
 
-        nc.sync.dma_start(lst[:], offs)
         nc.sync.dma_start(vlst[:], voffs)
+        nc.sync.dma_start(lst[:], offs)
+        vsc_rows = v_scales.bitcast(I32).rearrange("u f e -> f u e")
+        for g in range(4):
+            nc.sync.dma_start(
+                vsc_pool[32 * g + V_ROW : 32 * g + V_ROW + 4, :].rearrange("f (u e) -> f u e", u=POOL_PAGES),
+                vsc_rows[4 * g : 4 * g + 4],
+            )
         ks_rows = k_scales[0].bitcast(I32)
         for g in range(4):
             nc.sync.dma_start(ks_pool[32 * g : 32 * g + 4, :], ks_rows[4 * g : 4 * g + 4, :])
@@ -69,38 +68,24 @@ def tile_attend_pkv8_sigm_cap_kernel(tc, qT, k_words, k_scales, v_words, v_scale
         kw_pool = sb([P, T], I32, "kw_pool")
         nc.sync.dma_start(kw_pool[:], k_words[0].rearrange("p t r -> p (t r)").bitcast(I32))
 
-        q_bf = [sb([P, NQ, 4], BF16, "q_bf%d" % b, ("vw_pool", "vsc_pool")[b]) for b in range(B)]
+        q_bf = sb([P, B, NQ, 4], BF16, "q_bf", "vw_pool")
         for b in range(B):
-            nc.scalar.copy(q_bf[b][:], q_raw[:, b].rearrange("p j q -> p q j"))
+            nc.scalar.copy(q_bf[:, b], q_raw[:, b].rearrange("p j q -> p q j"))
         tok_pool = sb([P, T], F32, "tok_pool")
         nc.sync.dma_start(tok_pool[:], vs)
 
-        ks = [sb([P, N], U8, "ks%d" % b) for b in range(B)]
+        ks = sb([P, B * N], U8, "ks")
         q_codes = sb([P, B * NQ], U32, "q_codes")
         q_sc = sb([P, B * NQ], U8, "q_sc")
-
-        def gather_key_scales(b):
-            nc.vector.tensor_copy(ks[b][:], ks_pool[:].bitcast(U8).indirect(lst[:, b * 64 : (b + 1) * 64]))
-
-        gather_key_scales(0)
-        gather_key_scales(1)
-        for b in range(B):
-            cols = slice(b * NQ, (b + 1) * NQ)
-            nc.vector.quantize_mx(q_codes[:, cols].bitcast(FP8X4), q_sc[:, cols], q_bf[b][:].rearrange("p q j -> p (q j)"))
+        vsc = sb([P, PAGES * DV], U8, "vsc")
+        nc.vector.tensor_copy(vsc[:], vsc_pool[:].bitcast(U8).indirect(vlst[:]))
+        nc.vector.tensor_copy(ks[:], ks_pool[:].bitcast(U8).indirect(lst[:]))
+        nc.vector.quantize_mx(q_codes[:].bitcast(FP8X4), q_sc[:], q_bf[:].rearrange("p b q j -> p (b q j)"))
         vw_pool = sb([P, POOL_PAGES * DV], I32, "vw_pool")
         nc.sync.dma_start(
             vw_pool[:].rearrange("p (u e) -> p u e", u=POOL_PAGES),
             v_words.rearrange("u p e r -> p u (e r)").bitcast(I32),
         )
-
-        vsc_pool = sb([P, POOL_PAGES * DV // 4], I32, "vsc_pool")
-        nc.gpsimd.memset(vsc_pool[:], 0)
-        vsc_rows = v_scales.bitcast(I32).rearrange("u f e -> f u e")
-        for g in range(4):
-            nc.sync.dma_start(
-                vsc_pool[32 * g + V_ROW : 32 * g + V_ROW + 4, :].rearrange("f (u e) -> f u e", u=POOL_PAGES),
-                vsc_rows[4 * g : 4 * g + 4],
-            )
 
         kw = [sb([P, PAGE], U32, "kw%d" % e) for e in range(PAGES)]
         prob = [sb([P, PAGE], F32, "prob%d" % e) for e in range(PAGES)]
@@ -113,7 +98,7 @@ def tile_attend_pkv8_sigm_cap_kernel(tc, qT, k_words, k_scales, v_words, v_scale
                 lhsT=q_codes[:, b * NQ : (b + 1) * NQ].bitcast(FP8X4),
                 lhsT_scale=q_sc[:, b * NQ : (b + 1) * NQ],
                 rhs=kw[e][:].bitcast(FP8X4),
-                rhs_scale=ks[b][:, h * PAGE : (h + 1) * PAGE],
+                rhs_scale=ks[:, e * PAGE : (e + 1) * PAGE],
                 start=True,
                 stop=True,
             )
@@ -121,11 +106,10 @@ def tile_attend_pkv8_sigm_cap_kernel(tc, qT, k_words, k_scales, v_words, v_scale
             nc.scalar.activation(capped[:], sc[:], ACT.Sigmoid)
             nc.scalar.activation(prob[e][:], capped[:], ACT.Sigmoid, scale=4.0, bias=minus_two[:])
 
-        vsc = sb([P, PAGES * DV], U8, "vsc")
-        vw = [sb([P, DV], U32, "vw%d" % e) for e in range(PAGES)]
-        w_bf = [sb([P, NQ, 4], BF16, "w_bf%d" % e) for e in range(PAGES)]
-        w_codes = [sb([P, NQ], U32, "w_codes%d" % e) for e in range(PAGES)]
-        w_sc = [sb([P, NQ], U8, "w_sc%d" % e) for e in range(PAGES)]
+        vw = sb([P, PAGES * DV], U32, "vw")
+        w_bf = sb([P, PAGES, NQ, 4], BF16, "w_bf")
+        w_codes = sb([P, PAGES * NQ], U32, "w_codes")
+        w_sc = sb([P, PAGES * NQ], U8, "w_sc")
         y = [acc.tile([P, DV], F32, name="y%d" % b, tag="y") for b in range(B)]
 
         def weigh(e):
@@ -134,21 +118,26 @@ def tile_attend_pkv8_sigm_cap_kernel(tc, qT, k_words, k_scales, v_words, v_scale
             bank = turn.tile([P, 4, P], F32, name="bank", tag="turn")
             for t in range(4):
                 nc.tensor.transpose(bank[:, t, :], w[:, t::4], ident[:])
-            nc.scalar.copy(w_bf[e][:], bank[:].rearrange("p t q -> p q t"))
+            nc.scalar.copy(w_bf[:, e], bank[:].rearrange("p t q -> p q t"))
 
-        def gather_values(e):
-            nc.vector.tensor_copy(vw[e][:], vw_pool[:].bitcast(U32).indirect(vlst[:, e * 16 : (e + 1) * 16]))
+        def gather_values(first, last):
+            nc.vector.tensor_copy(
+                vw[:, first * DV : last * DV], vw_pool[:].bitcast(U32).indirect(vlst[:, first * 16 : last * 16])
+            )
 
-        def quantise_weights(e):
-            nc.vector.quantize_mx(w_codes[e][:].bitcast(FP8X4), w_sc[e][:], w_bf[e][:].rearrange("p q t -> p (q t)"))
+        def quantise_weights(first, last):
+            cols = slice(first * NQ, last * NQ)
+            nc.vector.quantize_mx(
+                w_codes[:, cols].bitcast(FP8X4), w_sc[:, cols], w_bf[:, first:last].rearrange("p e q t -> p (e q t)")
+            )
 
         def mix(e):
             b, h = divmod(e, N // PAGE)
             nc.tensor.matmul_mx(
                 y[b][:],
-                lhsT=w_codes[e][:].bitcast(FP8X4),
-                lhsT_scale=w_sc[e][:],
-                rhs=vw[e][:].bitcast(FP8X4),
+                lhsT=w_codes[:, e * NQ : (e + 1) * NQ].bitcast(FP8X4),
+                lhsT_scale=w_sc[:, e * NQ : (e + 1) * NQ],
+                rhs=vw[:, e * DV : (e + 1) * DV].bitcast(FP8X4),
                 rhs_scale=vsc[V_ROW:P, e * DV : (e + 1) * DV],
                 start=(h == 0),
                 stop=(h == 1),
@@ -160,8 +149,8 @@ def tile_attend_pkv8_sigm_cap_kernel(tc, qT, k_words, k_scales, v_words, v_scale
 
         for e in range(PAGES):
             weigh(e)
-        nc.vector.tensor_copy(vsc[:], vsc_pool[:].bitcast(U8).indirect(vlst[:]))
-        for e in range(PAGES):
-            quantise_weights(e)
-            gather_values(e)
-            mix(e)
+        for first, last in ((0, 2), (2, 3), (3, 4)):
+            quantise_weights(first, last)
+            gather_values(first, last)
+            for e in range(first, last):
+                mix(e)

@@ -15,13 +15,18 @@ ALU = mybir.AluOpType
 
 P = 128
 B, N, T, D, DV, NQ = 2, 1024, 4096, 512, 256, 128
-PAGE = 512
-PAGES = B * N // PAGE
+PACK = 4
+PAGE = P * PACK
+SEQ_PAGES = N // PAGE
+PAGES = B * SEQ_PAGES
 POOL_PAGES = T // PAGE
-V_ROW = 4
+LIST_ROWS = 16
+QUADRANTS, QUADRANT, SCALE_ROWS = 4, 32, 4
+VALUE_SCALE_ROW = 4
+MIX_RUNS = ((0, 2), (2, 3), (3, 4))
 
 FLOPS = 2 * B * NQ * N * (D + DV)
-BYTES = B * D * NQ * 4 + T * D + 16 * T + T * DV + 16 * POOL_PAGES * DV + T * 4 + P * (B * N + PAGES * DV) // 16 * 2 + B * NQ * DV * 4
+BYTES = 4 * B * D * NQ + (T * D + T * DV) * 33 // 32 + 4 * T + 2 * P * (B * N + PAGES * DV) // LIST_ROWS + 4 * B * NQ * DV
 
 
 def tile_attend_pkv8_sigm_cap_kernel(tc, qT, k_words, k_scales, v_words, v_scales, vs, offs, voffs, out):
@@ -30,15 +35,18 @@ def tile_attend_pkv8_sigm_cap_kernel(tc, qT, k_words, k_scales, v_words, v_scale
         keep = ctx.enter_context(tc.tile_pool(name="keep", bufs=1))
         turn = ctx.enter_context(tc.psum_pool(name="turn", bufs=3))
         score = ctx.enter_context(tc.psum_pool(name="score", bufs=3))
-        acc = ctx.enter_context(tc.psum_pool(name="acc", bufs=2))
+        acc = ctx.enter_context(tc.psum_pool(name="acc", bufs=B))
 
         def sb(shape, dtype, name, tag=None):
             return keep.tile(shape, dtype, name=name, tag=tag or name, align_bytes=64)
 
-        lst = keep.tile([P, B * N // 16], U16, name="lst")
-        vlst = keep.tile([P, PAGES * DV // 16], U16, name="vlst")
-        ks_pool = sb([P, T // 4], I32, "ks_pool")
-        vsc_pool = sb([P, POOL_PAGES * DV // 4], I32, "vsc_pool")
+        def entries(listing, first, last):
+            return listing[:, first // LIST_ROWS : last // LIST_ROWS]
+
+        lst = keep.tile([P, B * N // LIST_ROWS], U16, name="lst")
+        vlst = keep.tile([P, PAGES * DV // LIST_ROWS], U16, name="vlst")
+        ks_pool = sb([P, T // PACK], I32, "ks_pool")
+        vsc_pool = sb([P, POOL_PAGES * DV // PACK], I32, "vsc_pool")
         ident = sb([P, P], F32, "ident")
 
         one = sb([P, 1], F32, "one", "kw_pool")
@@ -49,28 +57,27 @@ def tile_attend_pkv8_sigm_cap_kernel(tc, qT, k_words, k_scales, v_words, v_scale
         nc.vector.memset(ks_pool[:], 0)
         nc.vector.tensor_scalar(minus_two[:], one[:], -2.0, None, ALU.mult)
 
-        warm = sb([P, 1], F32, "warm")
-        nc.scalar.activation(warm[:], minus_two[:], ACT.Sigmoid)
-
         nc.sync.dma_start(vlst[:], voffs)
         nc.sync.dma_start(lst[:], offs)
         vsc_rows = v_scales.bitcast(I32).rearrange("u f e -> f u e")
-        for g in range(4):
+        for g in range(QUADRANTS):
+            row = QUADRANT * g + VALUE_SCALE_ROW
             nc.sync.dma_start(
-                vsc_pool[32 * g + V_ROW : 32 * g + V_ROW + 4, :].rearrange("f (u e) -> f u e", u=POOL_PAGES),
-                vsc_rows[4 * g : 4 * g + 4],
+                vsc_pool[row : row + SCALE_ROWS, :].rearrange("f (u e) -> f u e", u=POOL_PAGES),
+                vsc_rows[SCALE_ROWS * g : SCALE_ROWS * (g + 1)],
             )
         ks_rows = k_scales[0].bitcast(I32)
-        for g in range(4):
-            nc.sync.dma_start(ks_pool[32 * g : 32 * g + 4, :], ks_rows[4 * g : 4 * g + 4, :])
-        q_raw = sb([P, B, 4, NQ], F32, "q_raw", "tok_pool")
-        nc.sync.dma_start(q_raw[:].rearrange("p b j q -> p b (j q)"), qT.rearrange("b (p j) q -> p b (j q)", j=4))
+        for g in range(QUADRANTS):
+            row = QUADRANT * g
+            nc.sync.dma_start(ks_pool[row : row + SCALE_ROWS, :], ks_rows[SCALE_ROWS * g : SCALE_ROWS * (g + 1), :])
+        q_raw = sb([P, B, PACK, NQ], F32, "q_raw", "tok_pool")
+        nc.sync.dma_start(q_raw[:].rearrange("p b t q -> p b (t q)"), qT.rearrange("b (p t) q -> p b (t q)", t=PACK))
         kw_pool = sb([P, T], I32, "kw_pool")
-        nc.sync.dma_start(kw_pool[:], k_words[0].rearrange("p t r -> p (t r)").bitcast(I32))
+        nc.sync.dma_start(kw_pool[:], k_words[0].rearrange("p n t -> p (n t)").bitcast(I32))
 
-        q_bf = sb([P, B, NQ, 4], BF16, "q_bf", "vw_pool")
+        q_bf = sb([P, B, NQ, PACK], BF16, "q_bf", "vw_pool")
         for b in range(B):
-            nc.scalar.copy(q_bf[:, b], q_raw[:, b].rearrange("p j q -> p q j"))
+            nc.scalar.copy(q_bf[:, b], q_raw[:, b].rearrange("p t q -> p q t"))
         tok_pool = sb([P, T], F32, "tok_pool")
         nc.sync.dma_start(tok_pool[:], vs)
 
@@ -80,77 +87,68 @@ def tile_attend_pkv8_sigm_cap_kernel(tc, qT, k_words, k_scales, v_words, v_scale
         vsc = sb([P, PAGES * DV], U8, "vsc")
         nc.vector.tensor_copy(vsc[:], vsc_pool[:].bitcast(U8).indirect(vlst[:]))
         nc.vector.tensor_copy(ks[:], ks_pool[:].bitcast(U8).indirect(lst[:]))
-        nc.vector.quantize_mx(q_codes[:].bitcast(FP8X4), q_sc[:], q_bf[:].rearrange("p b q j -> p (b q j)"))
+        nc.vector.quantize_mx(q_codes[:].bitcast(FP8X4), q_sc[:], q_bf[:].rearrange("p b q t -> p (b q t)"))
         vw_pool = sb([P, POOL_PAGES * DV], I32, "vw_pool")
         nc.sync.dma_start(
             vw_pool[:].rearrange("p (u e) -> p u e", u=POOL_PAGES),
-            v_words.rearrange("u p e r -> p u (e r)").bitcast(I32),
+            v_words.rearrange("u p e t -> p u (e t)").bitcast(I32),
         )
 
-        kw = [sb([P, PAGE], U32, "kw%d" % e) for e in range(PAGES)]
-        prob = [sb([P, PAGE], F32, "prob%d" % e) for e in range(PAGES)]
-        for e in range(PAGES):
-            b, h = divmod(e, N // PAGE)
-            nc.vector.tensor_copy(kw[e][:], kw_pool[:].bitcast(U32).indirect(lst[:, e * 32 : (e + 1) * 32]))
+        kw = [sb([P, PAGE], U32, "kw%d" % page) for page in range(PAGES)]
+        prob = [sb([P, PAGE], F32, "prob%d" % page) for page in range(PAGES)]
+        for page in range(PAGES):
+            queries = slice(page // SEQ_PAGES * NQ, (page // SEQ_PAGES + 1) * NQ)
+            tokens = entries(lst, page * PAGE, (page + 1) * PAGE)
+            nc.vector.tensor_copy(kw[page][:], kw_pool[:].bitcast(U32).indirect(tokens))
             sc = score.tile([P, PAGE], F32, name="sc")
             nc.tensor.matmul_mx(
                 sc[:],
-                lhsT=q_codes[:, b * NQ : (b + 1) * NQ].bitcast(FP8X4),
-                lhsT_scale=q_sc[:, b * NQ : (b + 1) * NQ],
-                rhs=kw[e][:].bitcast(FP8X4),
-                rhs_scale=ks[:, e * PAGE : (e + 1) * PAGE],
+                lhsT=q_codes[:, queries].bitcast(FP8X4),
+                lhsT_scale=q_sc[:, queries],
+                rhs=kw[page][:].bitcast(FP8X4),
+                rhs_scale=ks[:, page * PAGE : (page + 1) * PAGE],
                 start=True,
                 stop=True,
             )
-            capped = sb([P, PAGE], F32, "capped%d" % e)
-            nc.scalar.activation(capped[:], sc[:], ACT.Sigmoid)
-            nc.scalar.activation(prob[e][:], capped[:], ACT.Sigmoid, scale=4.0, bias=minus_two[:])
+            inner = sb([P, PAGE], F32, "inner%d" % page)
+            nc.scalar.activation(inner[:], sc[:], ACT.Sigmoid)
+            nc.scalar.activation(prob[page][:], inner[:], ACT.Sigmoid, scale=4.0, bias=minus_two[:])
 
         vw = sb([P, PAGES * DV], U32, "vw")
-        w_bf = sb([P, PAGES, NQ, 4], BF16, "w_bf")
+        w_bf = sb([P, PAGES, NQ, PACK], BF16, "w_bf")
         w_codes = sb([P, PAGES * NQ], U32, "w_codes")
         w_sc = sb([P, PAGES * NQ], U8, "w_sc")
         y = [acc.tile([P, DV], F32, name="y%d" % b, tag="y") for b in range(B)]
 
-        def weigh(e):
-            w = sb([P, PAGE], F32, "w%d" % e)
-            nc.vector.tensor_tensor(w[:], tok_pool[:].indirect(lst[:, e * 32 : (e + 1) * 32]), prob[e][:], ALU.mult)
-            bank = turn.tile([P, 4, P], F32, name="bank", tag="turn")
-            for t in range(4):
-                nc.tensor.transpose(bank[:, t, :], w[:, t::4], ident[:])
-            nc.scalar.copy(w_bf[:, e], bank[:].rearrange("p t q -> p q t"))
+        for page in range(PAGES):
+            w = sb([P, PAGE], F32, "w%d" % page)
+            tokens = entries(lst, page * PAGE, (page + 1) * PAGE)
+            nc.vector.tensor_tensor(w[:], tok_pool[:].indirect(tokens), prob[page][:], ALU.mult)
+            bank = turn.tile([P, PACK, NQ], F32, name="bank", tag="turn")
+            for t in range(PACK):
+                nc.tensor.transpose(bank[:, t, :], w[:, t::PACK], ident[:])
+            nc.scalar.copy(w_bf[:, page], bank[:].rearrange("p t q -> p q t"))
 
-        def gather_values(first, last):
-            nc.vector.tensor_copy(
-                vw[:, first * DV : last * DV], vw_pool[:].bitcast(U32).indirect(vlst[:, first * 16 : last * 16])
-            )
-
-        def quantise_weights(first, last):
+        for first, last in MIX_RUNS:
             cols = slice(first * NQ, last * NQ)
             nc.vector.quantize_mx(
-                w_codes[:, cols].bitcast(FP8X4), w_sc[:, cols], w_bf[:, first:last].rearrange("p e q t -> p (e q t)")
+                w_codes[:, cols].bitcast(FP8X4), w_sc[:, cols], w_bf[:, first:last].rearrange("p n q t -> p (n q t)")
             )
-
-        def mix(e):
-            b, h = divmod(e, N // PAGE)
-            nc.tensor.matmul_mx(
-                y[b][:],
-                lhsT=w_codes[:, e * NQ : (e + 1) * NQ].bitcast(FP8X4),
-                lhsT_scale=w_sc[:, e * NQ : (e + 1) * NQ],
-                rhs=vw[:, e * DV : (e + 1) * DV].bitcast(FP8X4),
-                rhs_scale=vsc[V_ROW:P, e * DV : (e + 1) * DV],
-                start=(h == 0),
-                stop=(h == 1),
+            nc.vector.tensor_copy(
+                vw[:, first * DV : last * DV], vw_pool[:].bitcast(U32).indirect(entries(vlst, first * DV, last * DV))
             )
-            if h == 1:
-                res = sb([P, DV], F32, "res%d" % b)
-                nc.scalar.activation(res[:], y[b][:], ACT.Copy, scale=1.0 / 16.0)
-                nc.sync.dma_start(out[b], res[:])
-
-        for e in range(PAGES):
-            weigh(e)
-        for first, last in ((0, 2), (2, 3), (3, 4)):
-            quantise_weights(first, last)
-            gather_values(first, last)
-            for e in range(first, last):
-                mix(e)
+            for page in range(first, last):
+                b, nth = divmod(page, SEQ_PAGES)
+                nc.tensor.matmul_mx(
+                    y[b][:],
+                    lhsT=w_codes[:, page * NQ : (page + 1) * NQ].bitcast(FP8X4),
+                    lhsT_scale=w_sc[:, page * NQ : (page + 1) * NQ],
+                    rhs=vw[:, page * DV : (page + 1) * DV].bitcast(FP8X4),
+                    rhs_scale=vsc[VALUE_SCALE_ROW:P, page * DV : (page + 1) * DV],
+                    start=(nth == 0),
+                    stop=(nth == SEQ_PAGES - 1),
+                )
+                if nth == SEQ_PAGES - 1:
+                    res = sb([P, DV], F32, "res%d" % b)
+                    nc.scalar.activation(res[:], y[b][:], ACT.Copy, scale=1.0 / 16.0)
+                    nc.sync.dma_start(out[b], res[:])

@@ -47,59 +47,61 @@ def tile_attend_pkv8_sigm_cap_kernel(tc, qT, k_words, k_scales, v_words, v_scale
         vlst = keep.tile([P, PAGES * DV // LIST_ROWS], U16, name="vlst")
         ks_pool = sb([P, T // PACK], I32, "ks_pool")
         vsc_pool = sb([P, POOL_PAGES * DV // PACK], I32, "vsc_pool")
+        tok_pool = sb([P, T], F32, "tok_pool")
+        tok_pages = tok_pool[:].rearrange("p (u c) -> p u c", u=POOL_PAGES)
         ident = sb([P, P], F32, "ident")
 
         one = sb([P, 1], F32, "one", "kw_pool")
         minus_two = sb([P, 1], F32, "minus_two")
         make_identity(nc, ident[:])
-        nc.vector.memset(vsc_pool[:], 0)
         nc.vector.memset(one[:], 1.0)
         nc.vector.memset(ks_pool[:], 0)
         nc.vector.tensor_scalar(minus_two[:], one[:], -2.0, None, ALU.mult)
+        nc.vector.memset(vsc_pool[:], 0)
+        nc.vector.memset(tok_pages[:, :, PACK:].bitcast(I32), 0)
 
-        nc.sync.dma_start(vlst[:], voffs)
         nc.sync.dma_start(lst[:], offs)
-        vsc_rows = v_scales.bitcast(I32).rearrange("u f e -> f u e")
-        for g in range(QUADRANTS):
-            row = QUADRANT * g + VALUE_SCALE_ROW
-            nc.sync.dma_start(
-                vsc_pool[row : row + SCALE_ROWS, :].rearrange("f (u e) -> f u e", u=POOL_PAGES),
-                vsc_rows[SCALE_ROWS * g : SCALE_ROWS * (g + 1)],
-            )
-        ks_rows = k_scales[0].bitcast(I32)
-        for g in range(QUADRANTS):
-            row = QUADRANT * g
-            nc.sync.dma_start(ks_pool[row : row + SCALE_ROWS, :], ks_rows[SCALE_ROWS * g : SCALE_ROWS * (g + 1), :])
-        q_raw = sb([P, B, PACK, NQ], F32, "q_raw", "tok_pool")
+        nc.sync.dma_start(vlst[:], voffs)
+        q_raw = sb([P, B, PACK, NQ], F32, "q_raw", "vw_pool")
         nc.sync.dma_start(q_raw[:].rearrange("p b t q -> p b (t q)"), qT.rearrange("b (p t) q -> p b (t q)", t=PACK))
+        nc.sync.dma_start(tok_pages[:, :, 0:PACK], vs[0].rearrange("(u p t) -> p u t", p=P, t=PACK))
+        ks_rows = k_scales[0].bitcast(I32).rearrange("(g r) c -> r g c", r=SCALE_ROWS)
+        for r in range(SCALE_ROWS):
+            nc.sync.dma_start(ks_pool[r:P:QUADRANT, :], ks_rows[r])
         kw_pool = sb([P, T], I32, "kw_pool")
         nc.sync.dma_start(kw_pool[:], k_words[0].rearrange("p n t -> p (n t)").bitcast(I32))
+        vsc_rows = v_scales.bitcast(I32).rearrange("u (g r) e -> r g u e", r=SCALE_ROWS)
+        for r in range(SCALE_ROWS):
+            nc.sync.dma_start(
+                vsc_pool[VALUE_SCALE_ROW + r : P : QUADRANT, :].rearrange("g (u e) -> g u e", u=POOL_PAGES), vsc_rows[r]
+            )
 
-        q_bf = sb([P, B, NQ, PACK], BF16, "q_bf", "vw_pool")
+        q_bf = sb([P, B, NQ, PACK], BF16, "q_bf")
         for b in range(B):
             nc.scalar.copy(q_bf[:, b], q_raw[:, b].rearrange("p t q -> p q t"))
-        tok_pool = sb([P, T], F32, "tok_pool")
-        nc.sync.dma_start(tok_pool[:], vs)
-
-        ks = sb([P, B * N], U8, "ks")
-        q_codes = sb([P, B * NQ], U32, "q_codes")
-        q_sc = sb([P, B * NQ], U8, "q_sc")
-        vsc = sb([P, PAGES * DV], U8, "vsc")
-        nc.vector.tensor_copy(vsc[:], vsc_pool[:].bitcast(U8).indirect(vlst[:]))
-        nc.vector.tensor_copy(ks[:], ks_pool[:].bitcast(U8).indirect(lst[:]))
-        nc.vector.quantize_mx(q_codes[:].bitcast(FP8X4), q_sc[:], q_bf[:].rearrange("p b q t -> p (b q t)"))
         vw_pool = sb([P, POOL_PAGES * DV], I32, "vw_pool")
         nc.sync.dma_start(
             vw_pool[:].rearrange("p (u e) -> p u e", u=POOL_PAGES),
             v_words.rearrange("u p e t -> p u (e t)").bitcast(I32),
         )
 
+        tok = sb([P, B * N], F32, "tok")
+        ks = sb([P, B * N], U8, "ks")
+        q_codes = sb([P, B * NQ], U32, "q_codes")
+        q_sc = sb([P, B * NQ], U8, "q_sc")
+        vsc = sb([P, PAGES * DV], U8, "vsc")
+        nc.vector.tensor_copy(tok[:], tok_pool[:].indirect(lst[:]))
+        nc.vector.tensor_copy(ks[:], ks_pool[:].bitcast(U8).indirect(lst[:]))
+        nc.vector.quantize_mx(q_codes[:].bitcast(FP8X4), q_sc[:], q_bf[:].rearrange("p b q t -> p (b q t)"))
+
         kw = [sb([P, PAGE], U32, "kw%d" % page) for page in range(PAGES)]
-        prob = [sb([P, PAGE], F32, "prob%d" % page) for page in range(PAGES)]
+        prob = [sb([P, NQ, PACK], F32, "prob%d" % page) for page in range(PAGES)]
         for page in range(PAGES):
-            queries = slice(page // SEQ_PAGES * NQ, (page // SEQ_PAGES + 1) * NQ)
             tokens = entries(lst, page * PAGE, (page + 1) * PAGE)
             nc.vector.tensor_copy(kw[page][:], kw_pool[:].bitcast(U32).indirect(tokens))
+        nc.vector.tensor_copy(vsc[:], vsc_pool[:].bitcast(U8).indirect(vlst[:]))
+        for page in range(PAGES):
+            queries = slice(page // SEQ_PAGES * NQ, (page // SEQ_PAGES + 1) * NQ)
             sc = score.tile([P, PAGE], F32, name="sc")
             nc.tensor.matmul_mx(
                 sc[:],
@@ -110,9 +112,14 @@ def tile_attend_pkv8_sigm_cap_kernel(tc, qT, k_words, k_scales, v_words, v_scale
                 start=True,
                 stop=True,
             )
-            inner = sb([P, PAGE], F32, "inner%d" % page)
-            nc.scalar.activation(inner[:], sc[:], ACT.Sigmoid)
-            nc.scalar.activation(prob[page][:], inner[:], ACT.Sigmoid, scale=4.0, bias=minus_two[:])
+            inner = sb([P, PACK, P], F32, "inner%d" % page)
+            nc.scalar.activation(inner[:], sc[:].rearrange("p (g t) -> p t g", t=PACK), ACT.Sigmoid)
+            bank = turn.tile([P, PACK, NQ], F32, name="bank", tag="turn")
+            for t in range(PACK):
+                nc.tensor.transpose(bank[:, t, :], inner[:, t, :], ident[:])
+            nc.scalar.activation(
+                prob[page][:], bank[:].rearrange("p t q -> p q t"), ACT.Sigmoid, scale=4.0, bias=minus_two[:]
+            )
 
         vw = sb([P, PAGES * DV], U32, "vw")
         w_bf = sb([P, PAGES, NQ, PACK], BF16, "w_bf")
@@ -120,22 +127,16 @@ def tile_attend_pkv8_sigm_cap_kernel(tc, qT, k_words, k_scales, v_words, v_scale
         w_sc = sb([P, PAGES * NQ], U8, "w_sc")
         y = [acc.tile([P, DV], F32, name="y%d" % b, tag="y") for b in range(B)]
 
-        for page in range(PAGES):
-            w = sb([P, PAGE], F32, "w%d" % page)
-            tokens = entries(lst, page * PAGE, (page + 1) * PAGE)
-            nc.vector.tensor_tensor(w[:], tok_pool[:].indirect(tokens), prob[page][:], ALU.mult)
-            bank = turn.tile([P, PACK, NQ], F32, name="bank", tag="turn")
-            for t in range(PACK):
-                nc.tensor.transpose(bank[:, t, :], w[:, t::PACK], ident[:])
-            nc.scalar.copy(w_bf[:, page], bank[:].rearrange("p t q -> p q t"))
-
         for first, last in MIX_RUNS:
+            for page in range(first, last):
+                scales = tok[:, page * PAGE : page * PAGE + PACK].unsqueeze(1).to_broadcast([P, NQ, PACK])
+                nc.vector.tensor_tensor(w_bf[:, page], prob[page][:], scales, ALU.mult)
+            nc.vector.tensor_copy(
+                vw[:, first * DV : last * DV], vw_pool[:].bitcast(U32).indirect(entries(vlst, first * DV, last * DV))
+            )
             cols = slice(first * NQ, last * NQ)
             nc.vector.quantize_mx(
                 w_codes[:, cols].bitcast(FP8X4), w_sc[:, cols], w_bf[:, first:last].rearrange("p n q t -> p (n q t)")
-            )
-            nc.vector.tensor_copy(
-                vw[:, first * DV : last * DV], vw_pool[:].bitcast(U32).indirect(entries(vlst, first * DV, last * DV))
             )
             for page in range(first, last):
                 b, nth = divmod(page, SEQ_PAGES)

@@ -54,17 +54,19 @@ def tile_attend_pkv8_sigm_cap_kernel(tc, qT, k_words, k_scales, v_words, v_scale
         one = sb([P, 1], F32, "one", "kw_pool")
         minus_two = sb([P, 1], F32, "minus_two")
         make_identity(nc, ident[:])
+        tok_rows = sb([P, PAGE], F32, "tok_rows")
+        nc.vector.memset(tok_rows[:].bitcast(I32), 0)
         nc.vector.memset(one[:], 1.0)
         nc.vector.memset(ks_pool[:], 0)
         nc.vector.tensor_scalar(minus_two[:], one[:], -2.0, None, ALU.mult)
         nc.vector.memset(vsc_pool[:], 0)
-        nc.vector.memset(tok_pages[:, :, PACK:].bitcast(I32), 0)
+        nc.vector.memset(tok_pool[:].bitcast(I32), 0)
 
         nc.sync.dma_start(lst[:], offs)
         nc.sync.dma_start(vlst[:], voffs)
         q_raw = sb([P, B, PACK, NQ], F32, "q_raw", "vw_pool")
         nc.sync.dma_start(q_raw[:].rearrange("p b t q -> p b (t q)"), qT.rearrange("b (p t) q -> p b (t q)", t=PACK))
-        nc.sync.dma_start(tok_pages[:, :, 0:PACK], vs[0].rearrange("(u p t) -> p u t", p=P, t=PACK))
+        nc.sync.dma_start(tok_rows[0:POOL_PAGES, :], vs[0].rearrange("(u c) -> u c", u=POOL_PAGES))
         ks_rows = k_scales[0].bitcast(I32).rearrange("(g r) c -> r g c", r=SCALE_ROWS)
         for r in range(SCALE_ROWS):
             nc.sync.dma_start(ks_pool[r:P:QUADRANT, :], ks_rows[r])
@@ -79,6 +81,10 @@ def tile_attend_pkv8_sigm_cap_kernel(tc, qT, k_words, k_scales, v_words, v_scale
         q_bf = sb([P, B, NQ, PACK], BF16, "q_bf")
         for b in range(B):
             nc.scalar.copy(q_bf[:, b], q_raw[:, b].rearrange("p t q -> p q t"))
+        bank = turn.tile([P, PACK, P], F32, name="bank", tag="turn")
+        for t in range(PACK):
+            nc.tensor.transpose(bank[:, t, :], tok_rows[:, t::PACK], ident[:])
+        nc.scalar.copy(tok_pages[:, :, 0:PACK], bank[:, :, 0:POOL_PAGES].rearrange("p t u -> p u t"))
         vw_pool = sb([P, POOL_PAGES * DV], I32, "vw_pool")
         nc.sync.dma_start(
             vw_pool[:].rearrange("p (u e) -> p u e", u=POOL_PAGES),
@@ -90,8 +96,8 @@ def tile_attend_pkv8_sigm_cap_kernel(tc, qT, k_words, k_scales, v_words, v_scale
         q_codes = sb([P, B * NQ], U32, "q_codes")
         q_sc = sb([P, B * NQ], U8, "q_sc")
         vsc = sb([P, PAGES * DV], U8, "vsc")
-        nc.vector.tensor_copy(tok[:], tok_pool[:].indirect(lst[:]))
         nc.vector.tensor_copy(ks[:], ks_pool[:].bitcast(U8).indirect(lst[:]))
+        nc.vector.tensor_copy(tok[:], tok_pool[:].indirect(lst[:]))
         nc.vector.quantize_mx(q_codes[:].bitcast(FP8X4), q_sc[:], q_bf[:].rearrange("p b q t -> p (b q t)"))
 
         kw = [sb([P, PAGE], U32, "kw%d" % page) for page in range(PAGES)]
@@ -113,7 +119,11 @@ def tile_attend_pkv8_sigm_cap_kernel(tc, qT, k_words, k_scales, v_words, v_scale
                 stop=True,
             )
             inner = sb([P, PACK, P], F32, "inner%d" % page)
-            nc.scalar.activation(inner[:], sc[:].rearrange("p (g t) -> p t g", t=PACK), ACT.Sigmoid)
+            nc.scalar.activation(
+                inner[:].rearrange("p t (c i) -> p c t i", i=PACK),
+                sc[:].rearrange("p (c i t) -> p c t i", i=PACK, t=PACK),
+                ACT.Sigmoid,
+            )
             bank = turn.tile([P, PACK, NQ], F32, name="bank", tag="turn")
             for t in range(PACK):
                 nc.tensor.transpose(bank[:, t, :], inner[:, t, :], ident[:])

@@ -51,25 +51,29 @@ def tile_attend_pkv8_sigm_cap_kernel(tc, qT, k_words, k_scales, v_words, v_scale
         tok_pages = tok_pool[:].rearrange("p (u c) -> p u c", u=POOL_PAGES)
         ident = sb([P, P], F32, "ident")
 
-        one = sb([P, 1], F32, "one", "kw_pool")
+        one = sb([P, 1], F32, "one", "q_raw")
+        two = sb([P, 1], F32, "two", "kw_pool")
         minus_two = sb([P, 1], F32, "minus_two")
         make_identity(nc, ident[:])
-        tok_rows = sb([P, PAGE], F32, "tok_rows")
-        nc.vector.memset(tok_rows[:].bitcast(I32), 0)
-        nc.vector.memset(one[:], 1.0)
+        tok_rows = sb([P, PAGE], F32, "tok_rows", "vw_pool")
+        nc.vector.memset(one[:], -1.0)
+        nc.vector.memset(two[:], 2.0)
         nc.vector.memset(ks_pool[:], 0)
-        nc.vector.tensor_scalar(minus_two[:], one[:], -2.0, None, ALU.mult)
+        nc.vector.memset(tok_rows[:].bitcast(I32), 0)
+        nc.vector.tensor_tensor(minus_two[:], one[:], two[:], ALU.mult)
+        warm = sb([P, 1], F32, "warm")
+        nc.scalar.activation(warm[:], minus_two[:], ACT.Sigmoid)
         nc.vector.memset(vsc_pool[:], 0)
         nc.vector.memset(tok_pool[:].bitcast(I32), 0)
 
         nc.sync.dma_start(lst[:], offs)
         nc.sync.dma_start(vlst[:], voffs)
-        q_raw = sb([P, B, PACK, NQ], F32, "q_raw", "vw_pool")
-        nc.sync.dma_start(q_raw[:].rearrange("p b t q -> p b (t q)"), qT.rearrange("b (p t) q -> p b (t q)", t=PACK))
-        nc.sync.dma_start(tok_rows[0:POOL_PAGES, :], vs[0].rearrange("(u c) -> u c", u=POOL_PAGES))
         ks_rows = k_scales[0].bitcast(I32).rearrange("(g r) c -> r g c", r=SCALE_ROWS)
         for r in range(SCALE_ROWS):
             nc.sync.dma_start(ks_pool[r:P:QUADRANT, :], ks_rows[r])
+        nc.sync.dma_start(tok_rows[0:POOL_PAGES, :], vs[0].rearrange("(u c) -> u c", u=POOL_PAGES))
+        q_raw = sb([P, B, PACK, NQ], F32, "q_raw")
+        nc.sync.dma_start(q_raw[:].rearrange("p b t q -> p b (t q)"), qT.rearrange("b (p t) q -> p b (t q)", t=PACK))
         kw_pool = sb([P, T], I32, "kw_pool")
         nc.sync.dma_start(kw_pool[:], k_words[0].rearrange("p n t -> p (n t)").bitcast(I32))
         vsc_rows = v_scales.bitcast(I32).rearrange("u (g r) e -> r g u e", r=SCALE_ROWS)
@@ -91,13 +95,11 @@ def tile_attend_pkv8_sigm_cap_kernel(tc, qT, k_words, k_scales, v_words, v_scale
             v_words.rearrange("u p e t -> p u (e t)").bitcast(I32),
         )
 
-        tok = sb([P, B * N], F32, "tok")
         ks = sb([P, B * N], U8, "ks")
         q_codes = sb([P, B * NQ], U32, "q_codes")
         q_sc = sb([P, B * NQ], U8, "q_sc")
         vsc = sb([P, PAGES * DV], U8, "vsc")
         nc.vector.tensor_copy(ks[:], ks_pool[:].bitcast(U8).indirect(lst[:]))
-        nc.vector.tensor_copy(tok[:], tok_pool[:].indirect(lst[:]))
         nc.vector.quantize_mx(q_codes[:].bitcast(FP8X4), q_sc[:], q_bf[:].rearrange("p b q t -> p (b q t)"))
 
         kw = [sb([P, PAGE], U32, "kw%d" % page) for page in range(PAGES)]
@@ -106,6 +108,11 @@ def tile_attend_pkv8_sigm_cap_kernel(tc, qT, k_words, k_scales, v_words, v_scale
             tokens = entries(lst, page * PAGE, (page + 1) * PAGE)
             nc.vector.tensor_copy(kw[page][:], kw_pool[:].bitcast(U32).indirect(tokens))
         nc.vector.tensor_copy(vsc[:], vsc_pool[:].bitcast(U8).indirect(vlst[:]))
+        tok = sb([P, B * N], F32, "tok", "kw_pool")
+        nc.vector.tensor_copy(tok[:], tok_pool[:].indirect(lst[:]))
+        vw = sb([P, PAGES * DV], U32, "vw")
+        nc.vector.tensor_copy(vw[:], vw_pool[:].bitcast(U32).indirect(vlst[:]))
+        inner = [sb([P, PACK, P], F32, "inner%d" % page) for page in range(PAGES)]
         for page in range(PAGES):
             queries = slice(page // SEQ_PAGES * NQ, (page // SEQ_PAGES + 1) * NQ)
             sc = score.tile([P, PAGE], F32, name="sc")
@@ -118,21 +125,20 @@ def tile_attend_pkv8_sigm_cap_kernel(tc, qT, k_words, k_scales, v_words, v_scale
                 start=True,
                 stop=True,
             )
-            inner = sb([P, PACK, P], F32, "inner%d" % page)
             nc.scalar.activation(
-                inner[:].rearrange("p t (c i) -> p c t i", i=PACK),
+                inner[page][:].rearrange("p t (c i) -> p c t i", i=PACK),
                 sc[:].rearrange("p (c i t) -> p c t i", i=PACK, t=PACK),
                 ACT.Sigmoid,
             )
+        for page in range(PAGES):
             bank = turn.tile([P, PACK, NQ], F32, name="bank", tag="turn")
             for t in range(PACK):
-                nc.tensor.transpose(bank[:, t, :], inner[:, t, :], ident[:])
+                nc.tensor.transpose(bank[:, t, :], inner[page][:, t, :], ident[:])
             nc.scalar.activation(
                 prob[page][:], bank[:].rearrange("p t q -> p q t"), ACT.Sigmoid, scale=4.0, bias=minus_two[:]
             )
 
-        vw = sb([P, PAGES * DV], U32, "vw")
-        w_bf = sb([P, PAGES, NQ, PACK], BF16, "w_bf")
+        w_bf = sb([P, PAGES, NQ, PACK], BF16, "w_bf", "vw_pool")
         w_codes = sb([P, PAGES * NQ], U32, "w_codes")
         w_sc = sb([P, PAGES * NQ], U8, "w_sc")
         y = [acc.tile([P, DV], F32, name="y%d" % b, tag="y") for b in range(B)]
@@ -141,9 +147,6 @@ def tile_attend_pkv8_sigm_cap_kernel(tc, qT, k_words, k_scales, v_words, v_scale
             for page in range(first, last):
                 scales = tok[:, page * PAGE : page * PAGE + PACK].unsqueeze(1).to_broadcast([P, NQ, PACK])
                 nc.vector.tensor_tensor(w_bf[:, page], prob[page][:], scales, ALU.mult)
-            nc.vector.tensor_copy(
-                vw[:, first * DV : last * DV], vw_pool[:].bitcast(U32).indirect(entries(vlst, first * DV, last * DV))
-            )
             cols = slice(first * NQ, last * NQ)
             nc.vector.quantize_mx(
                 w_codes[:, cols].bitcast(FP8X4), w_sc[:, cols], w_bf[:, first:last].rearrange("p n q t -> p (n q t)")

@@ -33,9 +33,8 @@ def tile_attend_pkv8_sigm_cap_kernel(tc, qT, k_words, k_scales, v_words, v_scale
     nc = tc.nc
     with ExitStack() as ctx:
         keep = ctx.enter_context(tc.tile_pool(name="keep", bufs=1))
-        turn = ctx.enter_context(tc.psum_pool(name="turn", bufs=3))
-        score = ctx.enter_context(tc.psum_pool(name="score", bufs=3))
-        acc = ctx.enter_context(tc.psum_pool(name="acc", bufs=B))
+        turn = ctx.enter_context(tc.psum_pool(name="turn", bufs=PAGES))
+        score = ctx.enter_context(tc.psum_pool(name="score", bufs=PAGES))
 
         def sb(shape, dtype, name, tag=None):
             return keep.tile(shape, dtype, name=name, tag=tag or name, align_bytes=64)
@@ -101,6 +100,8 @@ def tile_attend_pkv8_sigm_cap_kernel(tc, qT, k_words, k_scales, v_words, v_scale
         vsc = sb([P, PAGES * DV], U8, "vsc")
         nc.vector.tensor_copy(ks[:], ks_pool[:].bitcast(U8).indirect(lst[:]))
         nc.vector.quantize_mx(q_codes[:].bitcast(FP8X4), q_sc[:], q_bf[:].rearrange("p b q t -> p (b q t)"))
+        tok = sb([P, B * N], F32, "tok")
+        nc.vector.tensor_copy(tok[:], tok_pool[:].indirect(lst[:]))
 
         kw = [sb([P, PAGE], U32, "kw%d" % page) for page in range(PAGES)]
         prob = [sb([P, NQ, PACK], F32, "prob%d" % page) for page in range(PAGES)]
@@ -108,8 +109,6 @@ def tile_attend_pkv8_sigm_cap_kernel(tc, qT, k_words, k_scales, v_words, v_scale
             tokens = entries(lst, page * PAGE, (page + 1) * PAGE)
             nc.vector.tensor_copy(kw[page][:], kw_pool[:].bitcast(U32).indirect(tokens))
         nc.vector.tensor_copy(vsc[:], vsc_pool[:].bitcast(U8).indirect(vlst[:]))
-        tok = sb([P, B * N], F32, "tok", "kw_pool")
-        nc.vector.tensor_copy(tok[:], tok_pool[:].indirect(lst[:]))
         vw = sb([P, PAGES * DV], U32, "vw")
         nc.vector.tensor_copy(vw[:], vw_pool[:].bitcast(U32).indirect(vlst[:]))
         inner = [sb([P, PACK, P], F32, "inner%d" % page) for page in range(PAGES)]
@@ -141,7 +140,7 @@ def tile_attend_pkv8_sigm_cap_kernel(tc, qT, k_words, k_scales, v_words, v_scale
         w_bf = sb([P, PAGES, NQ, PACK], BF16, "w_bf", "vw_pool")
         w_codes = sb([P, PAGES * NQ], U32, "w_codes")
         w_sc = sb([P, PAGES * NQ], U8, "w_sc")
-        y = [acc.tile([P, DV], F32, name="y%d" % b, tag="y") for b in range(B)]
+        y = [score.tile([P, DV], F32, name="y%d" % b, tag="sc") for b in range(B)]
 
         for first, last in MIX_RUNS:
             for page in range(first, last):

@@ -52,16 +52,18 @@ def tile_attend_pkv8_sigm_cap_kernel(tc, qT, k_words, k_scales, v_words, v_scale
 
         one = sb([P, 1], F32, "one", "q_raw")
         two = sb([P, 1], F32, "two", "kw_pool")
-        minus_two = sb([P, 1], F32, "minus_two")
+        zero = sb([P, 1], F32, "zero")
+        half = sb([P, 1], F32, "half")
+        minus_two = sb([P, 1], F32, "minus_two", "w_codes")
         make_identity(nc, ident[:])
         tok_rows = sb([P, PAGE], F32, "tok_rows", "vw_pool")
-        nc.vector.memset(one[:], -1.0)
-        nc.vector.memset(two[:], 2.0)
+        nc.vector.memset(one[:], 1.0)
+        nc.vector.memset(two[:], 1.0)
         nc.vector.memset(ks_pool[:], 0)
         nc.vector.memset(tok_rows[:].bitcast(I32), 0)
-        nc.vector.tensor_tensor(minus_two[:], one[:], two[:], ALU.mult)
-        warm = sb([P, 1], F32, "warm")
-        nc.scalar.activation(warm[:], minus_two[:], ACT.Sigmoid)
+        nc.vector.tensor_tensor(zero[:], one[:], two[:], ALU.subtract)
+        nc.scalar.activation(half[:], zero[:], ACT.Sigmoid)
+        nc.scalar.activation(minus_two[:], half[:], ACT.Copy, scale=-4.0)
         nc.vector.memset(vsc_pool[:], 0)
         nc.vector.memset(tok_pool[:].bitcast(I32), 0)
 
@@ -99,9 +101,9 @@ def tile_attend_pkv8_sigm_cap_kernel(tc, qT, k_words, k_scales, v_words, v_scale
         q_sc = sb([P, B * NQ], U8, "q_sc")
         vsc = sb([P, PAGES * DV], U8, "vsc")
         nc.vector.tensor_copy(ks[:], ks_pool[:].bitcast(U8).indirect(lst[:]))
-        nc.vector.quantize_mx(q_codes[:].bitcast(FP8X4), q_sc[:], q_bf[:].rearrange("p b q t -> p (b q t)"))
         tok = sb([P, B * N], F32, "tok")
         nc.vector.tensor_copy(tok[:], tok_pool[:].indirect(lst[:]))
+        nc.vector.quantize_mx(q_codes[:].bitcast(FP8X4), q_sc[:], q_bf[:].rearrange("p b q t -> p (b q t)"))
 
         kw = [sb([P, PAGE], U32, "kw%d" % page) for page in range(PAGES)]
         prob = [sb([P, NQ, PACK], F32, "prob%d" % page) for page in range(PAGES)]
@@ -142,10 +144,11 @@ def tile_attend_pkv8_sigm_cap_kernel(tc, qT, k_words, k_scales, v_words, v_scale
         w_sc = sb([P, PAGES * NQ], U8, "w_sc")
         y = [score.tile([P, DV], F32, name="y%d" % b, tag="sc") for b in range(B)]
 
-        for first, last in MIX_RUNS:
-            for page in range(first, last):
-                scales = tok[:, page * PAGE : page * PAGE + PACK].unsqueeze(1).to_broadcast([P, NQ, PACK])
-                nc.vector.tensor_tensor(w_bf[:, page], prob[page][:], scales, ALU.mult)
+        def weigh(page):
+            scales = tok[:, page * PAGE : page * PAGE + PACK].unsqueeze(1).to_broadcast([P, NQ, PACK])
+            nc.vector.tensor_tensor(w_bf[:, page], prob[page][:], scales, ALU.mult)
+
+        def mix(first, last):
             cols = slice(first * NQ, last * NQ)
             nc.vector.quantize_mx(
                 w_codes[:, cols].bitcast(FP8X4), w_sc[:, cols], w_bf[:, first:last].rearrange("p n q t -> p (n q t)")
@@ -165,3 +168,10 @@ def tile_attend_pkv8_sigm_cap_kernel(tc, qT, k_words, k_scales, v_words, v_scale
                     res = sb([P, DV], F32, "res%d" % b)
                     nc.scalar.activation(res[:], y[b][:], ACT.Copy, scale=1.0 / 16.0)
                     nc.sync.dma_start(out[b], res[:])
+
+        for page in range(PAGES - 1):
+            weigh(page)
+        mix(0, SEQ_PAGES)
+        weigh(PAGES - 1)
+        for page in range(SEQ_PAGES, PAGES):
+            mix(page, page + 1)

@@ -59,16 +59,22 @@ def tile_attend_pkv8_sigm_cap_kernel(tc, qT, k_words, k_scales, v_words, v_scale
         tok_rows = sb([P, PAGE], F32, "tok_rows", "vw_pool")
         nc.vector.memset(one[:], 1.0)
         nc.vector.memset(two[:], 1.0)
+        nc.vector.memset(vsc_pool[:], 0)
         nc.vector.memset(ks_pool[:], 0)
         nc.vector.memset(tok_rows[:].bitcast(I32), 0)
         nc.vector.tensor_tensor(zero[:], one[:], two[:], ALU.subtract)
         nc.scalar.activation(half[:], zero[:], ACT.Sigmoid)
         nc.scalar.activation(minus_two[:], half[:], ACT.Copy, scale=-4.0)
-        nc.vector.memset(vsc_pool[:], 0)
-        nc.vector.memset(tok_pool[:].bitcast(I32), 0)
+        nc.vector.memset(tok_pool[:, 0 : T // 2 + 8].bitcast(I32), 0)
+        nc.gpsimd.memset(tok_pool[:, T // 2 : T].bitcast(I32), 0)
 
-        nc.sync.dma_start(lst[:], offs)
         nc.sync.dma_start(vlst[:], voffs)
+        nc.sync.dma_start(lst[:], offs)
+        vsc_rows = v_scales.bitcast(I32).rearrange("u (g r) e -> r g u e", r=SCALE_ROWS)
+        for r in range(SCALE_ROWS):
+            nc.sync.dma_start(
+                vsc_pool[VALUE_SCALE_ROW + r : P : QUADRANT, :].rearrange("g (u e) -> g u e", u=POOL_PAGES), vsc_rows[r]
+            )
         ks_rows = k_scales[0].bitcast(I32).rearrange("(g r) c -> r g c", r=SCALE_ROWS)
         for r in range(SCALE_ROWS):
             nc.sync.dma_start(ks_pool[r:P:QUADRANT, :], ks_rows[r])
@@ -77,11 +83,6 @@ def tile_attend_pkv8_sigm_cap_kernel(tc, qT, k_words, k_scales, v_words, v_scale
         nc.sync.dma_start(q_raw[:].rearrange("p b t q -> p b (t q)"), qT.rearrange("b (p t) q -> p b (t q)", t=PACK))
         kw_pool = sb([P, T], I32, "kw_pool")
         nc.sync.dma_start(kw_pool[:], k_words[0].rearrange("p n t -> p (n t)").bitcast(I32))
-        vsc_rows = v_scales.bitcast(I32).rearrange("u (g r) e -> r g u e", r=SCALE_ROWS)
-        for r in range(SCALE_ROWS):
-            nc.sync.dma_start(
-                vsc_pool[VALUE_SCALE_ROW + r : P : QUADRANT, :].rearrange("g (u e) -> g u e", u=POOL_PAGES), vsc_rows[r]
-            )
 
         q_bf = sb([P, B, NQ, PACK], BF16, "q_bf")
         for b in range(B):
@@ -100,6 +101,7 @@ def tile_attend_pkv8_sigm_cap_kernel(tc, qT, k_words, k_scales, v_words, v_scale
         q_codes = sb([P, B * NQ], U32, "q_codes")
         q_sc = sb([P, B * NQ], U8, "q_sc")
         vsc = sb([P, PAGES * DV], U8, "vsc")
+        nc.vector.tensor_copy(vsc[:], vsc_pool[:].bitcast(U8).indirect(vlst[:]))
         nc.vector.tensor_copy(ks[:], ks_pool[:].bitcast(U8).indirect(lst[:]))
         tok = sb([P, B * N], F32, "tok")
         nc.vector.tensor_copy(tok[:], tok_pool[:].indirect(lst[:]))
@@ -110,7 +112,6 @@ def tile_attend_pkv8_sigm_cap_kernel(tc, qT, k_words, k_scales, v_words, v_scale
         for page in range(PAGES):
             tokens = entries(lst, page * PAGE, (page + 1) * PAGE)
             nc.vector.tensor_copy(kw[page][:], kw_pool[:].bitcast(U32).indirect(tokens))
-        nc.vector.tensor_copy(vsc[:], vsc_pool[:].bitcast(U8).indirect(vlst[:]))
         vw = sb([P, PAGES * DV], U32, "vw")
         nc.vector.tensor_copy(vw[:], vw_pool[:].bitcast(U32).indirect(vlst[:]))
         inner = [sb([P, PACK, P], F32, "inner%d" % page) for page in range(PAGES)]

@@ -23,7 +23,7 @@ POOL_PAGES = T // PAGE
 LIST_ROWS = 16
 QUADRANTS, QUADRANT, SCALE_ROWS = 4, 32, 4
 VALUE_SCALE_ROW = 4
-MIX_RUNS = ((0, 2), (2, 3), (3, 4))
+ZEROED_PAGES = 4
 
 FLOPS = 2 * B * NQ * N * (D + DV)
 BYTES = 4 * B * D * NQ + (T * D + T * DV) * 33 // 32 + 4 * T + 2 * P * (B * N + PAGES * DV) // LIST_ROWS + 4 * B * NQ * DV
@@ -60,13 +60,12 @@ def tile_attend_pkv8_sigm_cap_kernel(tc, qT, k_words, k_scales, v_words, v_scale
         nc.vector.memset(one[:], 1.0)
         nc.vector.memset(two[:], 1.0)
         nc.vector.memset(vsc_pool[:], 0)
-        nc.vector.memset(ks_pool[:], 0)
         nc.vector.memset(tok_rows[:].bitcast(I32), 0)
+        nc.vector.memset(ks_pool[:], 0)
         nc.vector.tensor_tensor(zero[:], one[:], two[:], ALU.subtract)
         nc.scalar.activation(half[:], zero[:], ACT.Sigmoid)
         nc.scalar.activation(minus_two[:], half[:], ACT.Copy, scale=-4.0)
-        nc.vector.memset(tok_pool[:, 0 : T // 2 + 8].bitcast(I32), 0)
-        nc.gpsimd.memset(tok_pool[:, T // 2 : T].bitcast(I32), 0)
+        nc.vector.memset(tok_pool[:, 0 : ZEROED_PAGES * PAGE].bitcast(I32), 0)
 
         nc.sync.dma_start(vlst[:], voffs)
         nc.sync.dma_start(lst[:], offs)
@@ -75,22 +74,27 @@ def tile_attend_pkv8_sigm_cap_kernel(tc, qT, k_words, k_scales, v_words, v_scale
             nc.sync.dma_start(
                 vsc_pool[VALUE_SCALE_ROW + r : P : QUADRANT, :].rearrange("g (u e) -> g u e", u=POOL_PAGES), vsc_rows[r]
             )
+        nc.sync.dma_start(tok_rows[0:POOL_PAGES, :], vs[0].rearrange("(u c) -> u c", u=POOL_PAGES))
         ks_rows = k_scales[0].bitcast(I32).rearrange("(g r) c -> r g c", r=SCALE_ROWS)
         for r in range(SCALE_ROWS):
             nc.sync.dma_start(ks_pool[r:P:QUADRANT, :], ks_rows[r])
-        nc.sync.dma_start(tok_rows[0:POOL_PAGES, :], vs[0].rearrange("(u c) -> u c", u=POOL_PAGES))
         q_raw = sb([P, B, PACK, NQ], F32, "q_raw")
         nc.sync.dma_start(q_raw[:].rearrange("p b t q -> p b (t q)"), qT.rearrange("b (p t) q -> p b (t q)", t=PACK))
         kw_pool = sb([P, T], I32, "kw_pool")
         nc.sync.dma_start(kw_pool[:], k_words[0].rearrange("p n t -> p (n t)").bitcast(I32))
 
         q_bf = sb([P, B, NQ, PACK], BF16, "q_bf")
-        for b in range(B):
-            nc.scalar.copy(q_bf[:, b], q_raw[:, b].rearrange("p t q -> p q t"))
         bank = turn.tile([P, PACK, P], F32, name="bank", tag="turn")
         for t in range(PACK):
             nc.tensor.transpose(bank[:, t, :], tok_rows[:, t::PACK], ident[:])
-        nc.scalar.copy(tok_pages[:, :, 0:PACK], bank[:, :, 0:POOL_PAGES].rearrange("p t u -> p u t"))
+        turned = bank[:, :, 0:POOL_PAGES].rearrange("p t u -> p u t")
+        nc.scalar.copy(tok_pages[:, 0:ZEROED_PAGES, 0:PACK], turned[:, 0:ZEROED_PAGES])
+        nc.scalar.copy(
+            tok_pages[:, ZEROED_PAGES:].rearrange("p u (c t) -> p u c t", t=PACK),
+            turned[:, ZEROED_PAGES:].unsqueeze(2).to_broadcast([P, POOL_PAGES - ZEROED_PAGES, P, PACK]),
+        )
+        for b in range(B):
+            nc.scalar.copy(q_bf[:, b], q_raw[:, b].rearrange("p t q -> p q t"))
         vw_pool = sb([P, POOL_PAGES * DV], I32, "vw_pool")
         nc.sync.dma_start(
             vw_pool[:].rearrange("p (u e) -> p u e", u=POOL_PAGES),
@@ -103,7 +107,7 @@ def tile_attend_pkv8_sigm_cap_kernel(tc, qT, k_words, k_scales, v_words, v_scale
         vsc = sb([P, PAGES * DV], U8, "vsc")
         nc.vector.tensor_copy(vsc[:], vsc_pool[:].bitcast(U8).indirect(vlst[:]))
         nc.vector.tensor_copy(ks[:], ks_pool[:].bitcast(U8).indirect(lst[:]))
-        tok = sb([P, B * N], F32, "tok")
+        tok = sb([P, B * N], F32, "tok", "ks_pool")
         nc.vector.tensor_copy(tok[:], tok_pool[:].indirect(lst[:]))
         nc.vector.quantize_mx(q_codes[:].bitcast(FP8X4), q_sc[:], q_bf[:].rearrange("p b q t -> p (b q t)"))
 

@@ -23,7 +23,12 @@ POOL_PAGES = T // PAGE
 LIST_ROWS = 16
 QUADRANTS, QUADRANT, SCALE_ROWS = 4, 32, 4
 VALUE_SCALE_ROW = 4
+EARLY_TOK_PAGES = 3
 ZEROED_PAGES = 4
+PAGE_BYTES = 4 * PAGE
+Q_RAW_AT = PAGE_BYTES // 2
+TOK_LATE_AT = 2 * PAGE_BYTES
+INNER_AT = (0, PAGE_BYTES, 3 * PAGE_BYTES, 4 * PAGE_BYTES)
 
 FLOPS = 2 * B * NQ * N * (D + DV)
 BYTES = 4 * B * D * NQ + (T * D + T * DV) * 33 // 32 + 4 * T + 2 * P * (B * N + PAGES * DV) // LIST_ROWS + 4 * B * NQ * DV
@@ -33,11 +38,15 @@ def tile_attend_pkv8_sigm_cap_kernel(tc, qT, k_words, k_scales, v_words, v_scale
     nc = tc.nc
     with ExitStack() as ctx:
         keep = ctx.enter_context(tc.tile_pool(name="keep", bufs=1))
+        shared = ctx.enter_context(tc.tile_pool(name="shared", bufs=1))
         turn = ctx.enter_context(tc.psum_pool(name="turn", bufs=PAGES))
-        score = ctx.enter_context(tc.psum_pool(name="score", bufs=PAGES))
+        score = ctx.enter_context(tc.psum_pool(name="score", bufs=1))
 
         def sb(shape, dtype, name, tag=None):
             return keep.tile(shape, dtype, name=name, tag=tag or name, align_bytes=64)
+
+        def placed(shape, dtype, name, offset):
+            return shared.tile(shape, dtype, name=name, align_bytes=64, offset=offset)
 
         def entries(listing, first, last):
             return listing[:, first // LIST_ROWS : last // LIST_ROWS]
@@ -50,11 +59,11 @@ def tile_attend_pkv8_sigm_cap_kernel(tc, qT, k_words, k_scales, v_words, v_scale
         tok_pages = tok_pool[:].rearrange("p (u c) -> p u c", u=POOL_PAGES)
         ident = sb([P, P], F32, "ident")
 
-        one = sb([P, 1], F32, "one", "q_raw")
+        one = placed([P, 1], F32, "one", Q_RAW_AT)
         two = sb([P, 1], F32, "two", "kw_pool")
         zero = sb([P, 1], F32, "zero")
         half = sb([P, 1], F32, "half")
-        minus_two = sb([P, 1], F32, "minus_two", "w_codes")
+        minus_two = sb([P, 1], F32, "minus_two")
         make_identity(nc, ident[:])
         tok_rows = sb([P, PAGE], F32, "tok_rows", "vw_pool")
         nc.vector.memset(one[:], 1.0)
@@ -78,23 +87,25 @@ def tile_attend_pkv8_sigm_cap_kernel(tc, qT, k_words, k_scales, v_words, v_scale
         ks_rows = k_scales[0].bitcast(I32).rearrange("(g r) c -> r g c", r=SCALE_ROWS)
         for r in range(SCALE_ROWS):
             nc.sync.dma_start(ks_pool[r:P:QUADRANT, :], ks_rows[r])
-        q_raw = sb([P, B, PACK, NQ], F32, "q_raw")
-        nc.sync.dma_start(q_raw[:].rearrange("p b t q -> p b (t q)"), qT.rearrange("b (p t) q -> p b (t q)", t=PACK))
+        q_raw = placed([P, B, PACK, NQ], F32, "q_raw", Q_RAW_AT)
+        q_rows = qT.rearrange("b (p t) q -> b p (t q)", t=PACK)
+        nc.sync.dma_start(q_raw[:, 0].rearrange("p t q -> p (t q)"), q_rows[0])
         kw_pool = sb([P, T], I32, "kw_pool")
         nc.sync.dma_start(kw_pool[:], k_words[0].rearrange("p n t -> p (n t)").bitcast(I32))
+        nc.sync.dma_start(q_raw[:, 1].rearrange("p t q -> p (t q)"), q_rows[1])
 
-        q_bf = sb([P, B, NQ, PACK], BF16, "q_bf")
         bank = turn.tile([P, PACK, P], F32, name="bank", tag="turn")
         for t in range(PACK):
             nc.tensor.transpose(bank[:, t, :], tok_rows[:, t::PACK], ident[:])
-        turned = bank[:, :, 0:POOL_PAGES].rearrange("p t u -> p u t")
-        nc.scalar.copy(tok_pages[:, 0:ZEROED_PAGES, 0:PACK], turned[:, 0:ZEROED_PAGES])
+        by_page = bank[:, :, 0:POOL_PAGES].rearrange("p t u -> p u t")
+        nc.scalar.copy(tok_pages[:, 0:ZEROED_PAGES, 0:PACK], by_page[:, 0:ZEROED_PAGES])
         nc.scalar.copy(
             tok_pages[:, ZEROED_PAGES:].rearrange("p u (c t) -> p u c t", t=PACK),
-            turned[:, ZEROED_PAGES:].unsqueeze(2).to_broadcast([P, POOL_PAGES - ZEROED_PAGES, P, PACK]),
+            by_page[:, ZEROED_PAGES:].unsqueeze(2).to_broadcast([P, POOL_PAGES - ZEROED_PAGES, P, PACK]),
         )
+        q_bf = [sb([P, NQ, PACK], BF16, "q_bf%d" % b) for b in range(B)]
         for b in range(B):
-            nc.scalar.copy(q_bf[:, b], q_raw[:, b].rearrange("p t q -> p q t"))
+            nc.scalar.copy(q_bf[b][:], q_raw[:, b].rearrange("p t q -> p q t"))
         vw_pool = sb([P, POOL_PAGES * DV], I32, "vw_pool")
         nc.sync.dma_start(
             vw_pool[:].rearrange("p (u e) -> p u e", u=POOL_PAGES),
@@ -105,23 +116,29 @@ def tile_attend_pkv8_sigm_cap_kernel(tc, qT, k_words, k_scales, v_words, v_scale
         q_codes = sb([P, B * NQ], U32, "q_codes")
         q_sc = sb([P, B * NQ], U8, "q_sc")
         vsc = sb([P, PAGES * DV], U8, "vsc")
+
+        def quantise_queries(b):
+            cols = slice(b * NQ, (b + 1) * NQ)
+            nc.vector.quantize_mx(q_codes[:, cols].bitcast(FP8X4), q_sc[:, cols], q_bf[b][:].rearrange("p q t -> p (q t)"))
+
         nc.vector.tensor_copy(vsc[:], vsc_pool[:].bitcast(U8).indirect(vlst[:]))
         nc.vector.tensor_copy(ks[:], ks_pool[:].bitcast(U8).indirect(lst[:]))
-        tok = sb([P, B * N], F32, "tok", "ks_pool")
-        nc.vector.tensor_copy(tok[:], tok_pool[:].indirect(lst[:]))
-        nc.vector.quantize_mx(q_codes[:].bitcast(FP8X4), q_sc[:], q_bf[:].rearrange("p b q t -> p (b q t)"))
+        early = EARLY_TOK_PAGES * PAGE
+        tok = sb([P, early], F32, "tok", "ks_pool")
+        nc.vector.tensor_copy(tok[:], tok_pool[:].indirect(entries(lst, 0, early)))
+        quantise_queries(0)
 
         kw = [sb([P, PAGE], U32, "kw%d" % page) for page in range(PAGES)]
-        prob = [sb([P, NQ, PACK], F32, "prob%d" % page) for page in range(PAGES)]
         for page in range(PAGES):
             tokens = entries(lst, page * PAGE, (page + 1) * PAGE)
             nc.vector.tensor_copy(kw[page][:], kw_pool[:].bitcast(U32).indirect(tokens))
-        vw = sb([P, PAGES * DV], U32, "vw")
-        nc.vector.tensor_copy(vw[:], vw_pool[:].bitcast(U32).indirect(vlst[:]))
-        inner = [sb([P, PACK, P], F32, "inner%d" % page) for page in range(PAGES)]
-        for page in range(PAGES):
+        quantise_queries(1)
+        inner = [placed([P, PACK, P], F32, "inner%d" % page, INNER_AT[page]) for page in range(PAGES)]
+        prob = [None] * PAGES
+
+        def inner_sigmoid(page):
             queries = slice(page // SEQ_PAGES * NQ, (page // SEQ_PAGES + 1) * NQ)
-            sc = score.tile([P, PAGE], F32, name="sc")
+            sc = score.tile([P, PAGE], F32, name="sc%d" % page)
             nc.tensor.matmul_mx(
                 sc[:],
                 lhsT=q_codes[:, queries].bitcast(FP8X4),
@@ -136,47 +153,58 @@ def tile_attend_pkv8_sigm_cap_kernel(tc, qT, k_words, k_scales, v_words, v_scale
                 sc[:].rearrange("p (c i t) -> p c t i", i=PACK, t=PACK),
                 ACT.Sigmoid,
             )
-        for page in range(PAGES):
+
+        def turned(dealt):
             bank = turn.tile([P, PACK, NQ], F32, name="bank", tag="turn")
             for t in range(PACK):
-                nc.tensor.transpose(bank[:, t, :], inner[page][:, t, :], ident[:])
-            nc.scalar.activation(
-                prob[page][:], bank[:].rearrange("p t q -> p q t"), ACT.Sigmoid, scale=4.0, bias=minus_two[:]
-            )
+                nc.tensor.transpose(bank[:, t, :], dealt[:, t, :], ident[:])
+            return bank[:].rearrange("p t q -> p q t")
+
+        def outer_then_turn(page):
+            outer = sb([P, PACK, P], F32, "outer%d" % page)
+            nc.scalar.activation(outer[:], inner[page][:], ACT.Sigmoid, scale=4.0, bias=minus_two[:])
+            prob[page] = turned(outer)
+
+        def turn_then_outer(page):
+            outer = sb([P, NQ, PACK], F32, "outer%d" % page)
+            nc.scalar.activation(outer[:], turned(inner[page]), ACT.Sigmoid, scale=4.0, bias=minus_two[:])
+            prob[page] = outer[:]
+
+        for b, finish in enumerate((outer_then_turn, turn_then_outer)):
+            for page in range(b * SEQ_PAGES, (b + 1) * SEQ_PAGES):
+                inner_sigmoid(page)
+            for page in range(b * SEQ_PAGES, (b + 1) * SEQ_PAGES):
+                finish(page)
+
+        tok_late = placed([P, B * N - early], F32, "tok_late", TOK_LATE_AT)
+        nc.vector.tensor_copy(tok_late[:], tok_pool[:].indirect(entries(lst, early, B * N)))
+        vw = sb([P, PAGES * DV], U32, "vw")
+        nc.vector.tensor_copy(vw[:], vw_pool[:].bitcast(U32).indirect(vlst[:]))
 
         w_bf = sb([P, PAGES, NQ, PACK], BF16, "w_bf", "vw_pool")
         w_codes = sb([P, PAGES * NQ], U32, "w_codes")
         w_sc = sb([P, PAGES * NQ], U8, "w_sc")
-        y = [score.tile([P, DV], F32, name="y%d" % b, tag="sc") for b in range(B)]
+        y = [score.tile([P, DV], F32, name="y%d" % b, tag="sc%d" % (PAGES - 1 - b)) for b in range(B)]
 
-        def weigh(page):
-            scales = tok[:, page * PAGE : page * PAGE + PACK].unsqueeze(1).to_broadcast([P, NQ, PACK])
-            nc.vector.tensor_tensor(w_bf[:, page], prob[page][:], scales, ALU.mult)
-
-        def mix(first, last):
-            cols = slice(first * NQ, last * NQ)
+        for page in range(PAGES):
+            held, first = (tok, 0) if page < EARLY_TOK_PAGES else (tok_late, EARLY_TOK_PAGES)
+            scales = held[:, (page - first) * PAGE : (page - first) * PAGE + PACK].unsqueeze(1).to_broadcast([P, NQ, PACK])
+            nc.vector.tensor_tensor(w_bf[:, page], prob[page], scales, ALU.mult)
+            cols = slice(page * NQ, (page + 1) * NQ)
             nc.vector.quantize_mx(
-                w_codes[:, cols].bitcast(FP8X4), w_sc[:, cols], w_bf[:, first:last].rearrange("p n q t -> p (n q t)")
+                w_codes[:, cols].bitcast(FP8X4), w_sc[:, cols], w_bf[:, page].rearrange("p q t -> p (q t)")
             )
-            for page in range(first, last):
-                b, nth = divmod(page, SEQ_PAGES)
-                nc.tensor.matmul_mx(
-                    y[b][:],
-                    lhsT=w_codes[:, page * NQ : (page + 1) * NQ].bitcast(FP8X4),
-                    lhsT_scale=w_sc[:, page * NQ : (page + 1) * NQ],
-                    rhs=vw[:, page * DV : (page + 1) * DV].bitcast(FP8X4),
-                    rhs_scale=vsc[VALUE_SCALE_ROW:P, page * DV : (page + 1) * DV],
-                    start=(nth == 0),
-                    stop=(nth == SEQ_PAGES - 1),
-                )
-                if nth == SEQ_PAGES - 1:
-                    res = sb([P, DV], F32, "res%d" % b)
-                    nc.scalar.activation(res[:], y[b][:], ACT.Copy, scale=1.0 / 16.0)
-                    nc.sync.dma_start(out[b], res[:])
-
-        for page in range(PAGES - 1):
-            weigh(page)
-        mix(0, SEQ_PAGES)
-        weigh(PAGES - 1)
-        for page in range(SEQ_PAGES, PAGES):
-            mix(page, page + 1)
+            b, nth = divmod(page, SEQ_PAGES)
+            nc.tensor.matmul_mx(
+                y[b][:],
+                lhsT=w_codes[:, cols].bitcast(FP8X4),
+                lhsT_scale=w_sc[:, cols],
+                rhs=vw[:, page * DV : (page + 1) * DV].bitcast(FP8X4),
+                rhs_scale=vsc[VALUE_SCALE_ROW:P, page * DV : (page + 1) * DV],
+                start=(nth == 0),
+                stop=(nth == SEQ_PAGES - 1),
+            )
+            if nth == SEQ_PAGES - 1:
+                res = sb([P, DV], F32, "res%d" % b)
+                nc.scalar.activation(res[:], y[b][:], ACT.Copy, scale=1.0 / 16.0)
+                nc.sync.dma_start(out[b], res[:])

@@ -23,12 +23,10 @@ POOL_PAGES = T // PAGE
 LIST_ROWS = 16
 QUADRANTS, QUADRANT, SCALE_ROWS = 4, 32, 4
 VALUE_SCALE_ROW = 4
-EARLY_TOK_PAGES = 3
+EARLY_TOK_PAGES = 2
 ZEROED_PAGES = 4
-PAGE_BYTES = 4 * PAGE
-Q_RAW_AT = PAGE_BYTES // 2
-TOK_LATE_AT = 2 * PAGE_BYTES
-INNER_AT = (0, PAGE_BYTES, 3 * PAGE_BYTES, 4 * PAGE_BYTES)
+CODE_BYTES = 4 * NQ
+OUTER_AT = (16 * CODE_BYTES, 0)
 
 FLOPS = 2 * B * NQ * N * (D + DV)
 BYTES = 4 * B * D * NQ + (T * D + T * DV) * 33 // 32 + 4 * T + 2 * P * (B * N + PAGES * DV) // LIST_ROWS + 4 * B * NQ * DV
@@ -59,19 +57,18 @@ def tile_attend_pkv8_sigm_cap_kernel(tc, qT, k_words, k_scales, v_words, v_scale
         tok_pages = tok_pool[:].rearrange("p (u c) -> p u c", u=POOL_PAGES)
         ident = sb([P, P], F32, "ident")
 
-        one = placed([P, 1], F32, "one", Q_RAW_AT)
-        two = sb([P, 1], F32, "two", "kw_pool")
+        ones = [sb([P, 1], F32, "one_" + tag, tag) for tag in ("q_raw0", "kw_pool", "q_raw1")]
         zero = sb([P, 1], F32, "zero")
         half = sb([P, 1], F32, "half")
         minus_two = sb([P, 1], F32, "minus_two")
+        nc.gpsimd.memset(vsc_pool[:], 0)
         make_identity(nc, ident[:])
         tok_rows = sb([P, PAGE], F32, "tok_rows", "vw_pool")
-        nc.vector.memset(one[:], 1.0)
-        nc.vector.memset(two[:], 1.0)
-        nc.vector.memset(vsc_pool[:], 0)
         nc.vector.memset(tok_rows[:].bitcast(I32), 0)
         nc.vector.memset(ks_pool[:], 0)
-        nc.vector.tensor_tensor(zero[:], one[:], two[:], ALU.subtract)
+        for one in ones:
+            nc.vector.memset(one[:], 1.0)
+        nc.vector.tensor_scalar(zero[:], ones[0][:], ones[1][:], ones[2][:], ALU.subtract, ALU.mult)
         nc.scalar.activation(half[:], zero[:], ACT.Sigmoid)
         nc.scalar.activation(minus_two[:], half[:], ACT.Copy, scale=-4.0)
         nc.vector.memset(tok_pool[:, 0 : ZEROED_PAGES * PAGE].bitcast(I32), 0)
@@ -83,16 +80,16 @@ def tile_attend_pkv8_sigm_cap_kernel(tc, qT, k_words, k_scales, v_words, v_scale
             nc.sync.dma_start(
                 vsc_pool[VALUE_SCALE_ROW + r : P : QUADRANT, :].rearrange("g (u e) -> g u e", u=POOL_PAGES), vsc_rows[r]
             )
-        nc.sync.dma_start(tok_rows[0:POOL_PAGES, :], vs[0].rearrange("(u c) -> u c", u=POOL_PAGES))
         ks_rows = k_scales[0].bitcast(I32).rearrange("(g r) c -> r g c", r=SCALE_ROWS)
         for r in range(SCALE_ROWS):
             nc.sync.dma_start(ks_pool[r:P:QUADRANT, :], ks_rows[r])
-        q_raw = placed([P, B, PACK, NQ], F32, "q_raw", Q_RAW_AT)
+        nc.gpsimd.dma_start(tok_rows[0:POOL_PAGES, :], vs[0].rearrange("(u c) -> u c", u=POOL_PAGES))
+        q_raw = [sb([P, PACK, NQ], F32, "q_raw%d" % b) for b in range(B)]
         q_rows = qT.rearrange("b (p t) q -> b p (t q)", t=PACK)
-        nc.sync.dma_start(q_raw[:, 0].rearrange("p t q -> p (t q)"), q_rows[0])
+        nc.sync.dma_start(q_raw[0][:].rearrange("p t q -> p (t q)"), q_rows[0])
         kw_pool = sb([P, T], I32, "kw_pool")
         nc.sync.dma_start(kw_pool[:], k_words[0].rearrange("p n t -> p (n t)").bitcast(I32))
-        nc.sync.dma_start(q_raw[:, 1].rearrange("p t q -> p (t q)"), q_rows[1])
+        nc.sync.dma_start(q_raw[1][:].rearrange("p t q -> p (t q)"), q_rows[1])
 
         bank = turn.tile([P, PACK, P], F32, name="bank", tag="turn")
         for t in range(PACK):
@@ -105,7 +102,9 @@ def tile_attend_pkv8_sigm_cap_kernel(tc, qT, k_words, k_scales, v_words, v_scale
         )
         q_bf = [sb([P, NQ, PACK], BF16, "q_bf%d" % b) for b in range(B)]
         for b in range(B):
-            nc.scalar.copy(q_bf[b][:], q_raw[:, b].rearrange("p t q -> p q t"))
+            nc.scalar.copy(
+                q_bf[b][:].rearrange("p (c i) t -> p c t i", i=PACK), q_raw[b][:].rearrange("p t (c i) -> p c t i", i=PACK)
+            )
         vw_pool = sb([P, POOL_PAGES * DV], I32, "vw_pool")
         nc.sync.dma_start(
             vw_pool[:].rearrange("p (u e) -> p u e", u=POOL_PAGES),
@@ -124,7 +123,7 @@ def tile_attend_pkv8_sigm_cap_kernel(tc, qT, k_words, k_scales, v_words, v_scale
         nc.vector.tensor_copy(vsc[:], vsc_pool[:].bitcast(U8).indirect(vlst[:]))
         nc.vector.tensor_copy(ks[:], ks_pool[:].bitcast(U8).indirect(lst[:]))
         early = EARLY_TOK_PAGES * PAGE
-        tok = sb([P, early], F32, "tok", "ks_pool")
+        tok = sb([P, early], F32, "tok", "q_raw0")
         nc.vector.tensor_copy(tok[:], tok_pool[:].indirect(entries(lst, 0, early)))
         quantise_queries(0)
 
@@ -133,7 +132,7 @@ def tile_attend_pkv8_sigm_cap_kernel(tc, qT, k_words, k_scales, v_words, v_scale
             tokens = entries(lst, page * PAGE, (page + 1) * PAGE)
             nc.vector.tensor_copy(kw[page][:], kw_pool[:].bitcast(U32).indirect(tokens))
         quantise_queries(1)
-        inner = [placed([P, PACK, P], F32, "inner%d" % page, INNER_AT[page]) for page in range(PAGES)]
+        inner = [sb([P, PACK, P], F32, "inner%d" % page) for page in range(PAGES)]
         prob = [None] * PAGES
 
         def inner_sigmoid(page):
@@ -161,7 +160,7 @@ def tile_attend_pkv8_sigm_cap_kernel(tc, qT, k_words, k_scales, v_words, v_scale
             return bank[:].rearrange("p t q -> p q t")
 
         def outer_then_turn(page):
-            outer = sb([P, PACK, P], F32, "outer%d" % page)
+            outer = placed([P, PACK, P], F32, "outer%d" % page, OUTER_AT[page])
             nc.scalar.activation(outer[:], inner[page][:], ACT.Sigmoid, scale=4.0, bias=minus_two[:])
             prob[page] = turned(outer)
 
@@ -176,28 +175,36 @@ def tile_attend_pkv8_sigm_cap_kernel(tc, qT, k_words, k_scales, v_words, v_scale
             for page in range(b * SEQ_PAGES, (b + 1) * SEQ_PAGES):
                 finish(page)
 
-        tok_late = placed([P, B * N - early], F32, "tok_late", TOK_LATE_AT)
+        tok_late = sb([P, B * N - early], F32, "tok_late", "q_raw1")
         nc.vector.tensor_copy(tok_late[:], tok_pool[:].indirect(entries(lst, early, B * N)))
         vw = sb([P, PAGES * DV], U32, "vw")
         nc.vector.tensor_copy(vw[:], vw_pool[:].bitcast(U32).indirect(vlst[:]))
 
-        w_bf = sb([P, PAGES, NQ, PACK], BF16, "w_bf", "vw_pool")
-        w_codes = sb([P, PAGES * NQ], U32, "w_codes")
+        w_all = sb([P, PAGES, NQ, PACK], BF16, "w_bf", "vw_pool")
+        w_bf = [w_all[:, page] for page in range(PAGES)]
+        w_codes = [
+            placed([P, NQ], U32, "w_codes0", 0),
+            sb([P, NQ], U32, "w_codes1"),
+            sb([P, NQ], U32, "w_codes2", "minus_two"),
+            sb([P, NQ], U32, "w_codes3"),
+        ]
         w_sc = sb([P, PAGES * NQ], U8, "w_sc")
         y = [score.tile([P, DV], F32, name="y%d" % b, tag="sc%d" % (PAGES - 1 - b)) for b in range(B)]
 
-        for page in range(PAGES):
+        def product(page):
             held, first = (tok, 0) if page < EARLY_TOK_PAGES else (tok_late, EARLY_TOK_PAGES)
             scales = held[:, (page - first) * PAGE : (page - first) * PAGE + PACK].unsqueeze(1).to_broadcast([P, NQ, PACK])
-            nc.vector.tensor_tensor(w_bf[:, page], prob[page], scales, ALU.mult)
+            nc.vector.tensor_tensor(w_bf[page], prob[page], scales, ALU.mult)
+
+        def weigh_values(page):
             cols = slice(page * NQ, (page + 1) * NQ)
             nc.vector.quantize_mx(
-                w_codes[:, cols].bitcast(FP8X4), w_sc[:, cols], w_bf[:, page].rearrange("p q t -> p (q t)")
+                w_codes[page][:].bitcast(FP8X4), w_sc[:, cols], w_bf[page].rearrange("p q t -> p (q t)")
             )
             b, nth = divmod(page, SEQ_PAGES)
             nc.tensor.matmul_mx(
                 y[b][:],
-                lhsT=w_codes[:, cols].bitcast(FP8X4),
+                lhsT=w_codes[page][:].bitcast(FP8X4),
                 lhsT_scale=w_sc[:, cols],
                 rhs=vw[:, page * DV : (page + 1) * DV].bitcast(FP8X4),
                 rhs_scale=vsc[VALUE_SCALE_ROW:P, page * DV : (page + 1) * DV],
@@ -208,3 +215,12 @@ def tile_attend_pkv8_sigm_cap_kernel(tc, qT, k_words, k_scales, v_words, v_scale
                 res = sb([P, DV], F32, "res%d" % b)
                 nc.scalar.activation(res[:], y[b][:], ACT.Copy, scale=1.0 / 16.0)
                 nc.sync.dma_start(out[b], res[:])
+
+        product(0)
+        product(1)
+        weigh_values(0)
+        product(2)
+        weigh_values(1)
+        product(3)
+        weigh_values(2)
+        weigh_values(3)

@@ -80,10 +80,10 @@ def tile_attend_pkv8_sigm_cap_kernel(tc, qT, k_words, k_scales, v_words, v_scale
             nc.sync.dma_start(
                 vsc_pool[VALUE_SCALE_ROW + r : P : QUADRANT, :].rearrange("g (u e) -> g u e", u=POOL_PAGES), vsc_rows[r]
             )
+        nc.sync.dma_start(tok_rows[0:POOL_PAGES, :], vs[0].rearrange("(u c) -> u c", u=POOL_PAGES))
         ks_rows = k_scales[0].bitcast(I32).rearrange("(g r) c -> r g c", r=SCALE_ROWS)
         for r in range(SCALE_ROWS):
             nc.sync.dma_start(ks_pool[r:P:QUADRANT, :], ks_rows[r])
-        nc.gpsimd.dma_start(tok_rows[0:POOL_PAGES, :], vs[0].rearrange("(u c) -> u c", u=POOL_PAGES))
         q_raw = [sb([P, PACK, NQ], F32, "q_raw%d" % b) for b in range(B)]
         q_rows = qT.rearrange("b (p t) q -> b p (t q)", t=PACK)
         nc.sync.dma_start(q_raw[0][:].rearrange("p t q -> p (t q)"), q_rows[0])

@@ -23,7 +23,7 @@ POOL_PAGES = T // PAGE
 LIST_ROWS = 16
 QUADRANTS, QUADRANT, SCALE_ROWS = 4, 32, 4
 VALUE_SCALE_ROW = 4
-EARLY_TOK_PAGES = 2
+EARLY_TOK_PAGES = 3
 ZEROED_PAGES = 4
 CODE_BYTES = 4 * NQ
 OUTER_AT = (16 * CODE_BYTES, 0)
@@ -55,23 +55,24 @@ def tile_attend_pkv8_sigm_cap_kernel(tc, qT, k_words, k_scales, v_words, v_scale
         vsc_pool = sb([P, POOL_PAGES * DV // PACK], I32, "vsc_pool")
         tok_pool = sb([P, T], F32, "tok_pool")
         tok_pages = tok_pool[:].rearrange("p (u c) -> p u c", u=POOL_PAGES)
-        ident = sb([P, P], F32, "ident")
 
-        ones = [sb([P, 1], F32, "one_" + tag, tag) for tag in ("q_raw0", "kw_pool", "q_raw1")]
+        ones = [sb([P, 1], F32, "one_" + tag, tag) for tag in ("q_raw", "kw_pool", "ident")]
         zero = sb([P, 1], F32, "zero")
         half = sb([P, 1], F32, "half")
         minus_two = sb([P, 1], F32, "minus_two")
-        nc.gpsimd.memset(vsc_pool[:], 0)
-        make_identity(nc, ident[:])
         tok_rows = sb([P, PAGE], F32, "tok_rows", "vw_pool")
-        nc.vector.memset(tok_rows[:].bitcast(I32), 0)
+        nc.vector.memset(vsc_pool[:], 0)
         nc.vector.memset(ks_pool[:], 0)
+        nc.vector.memset(tok_rows[:].bitcast(I32), 0)
         for one in ones:
             nc.vector.memset(one[:], 1.0)
         nc.vector.tensor_scalar(zero[:], ones[0][:], ones[1][:], ones[2][:], ALU.subtract, ALU.mult)
+        ident = sb([P, P], F32, "ident")
+        make_identity(nc, ident[:])
         nc.scalar.activation(half[:], zero[:], ACT.Sigmoid)
         nc.scalar.activation(minus_two[:], half[:], ACT.Copy, scale=-4.0)
-        nc.vector.memset(tok_pool[:, 0 : ZEROED_PAGES * PAGE].bitcast(I32), 0)
+        for first in range(0, ZEROED_PAGES, 2):
+            nc.vector.memset(tok_pages[:, first : first + 2].bitcast(I32), 0)
 
         nc.sync.dma_start(vlst[:], voffs)
         nc.sync.dma_start(lst[:], offs)
@@ -80,30 +81,30 @@ def tile_attend_pkv8_sigm_cap_kernel(tc, qT, k_words, k_scales, v_words, v_scale
             nc.sync.dma_start(
                 vsc_pool[VALUE_SCALE_ROW + r : P : QUADRANT, :].rearrange("g (u e) -> g u e", u=POOL_PAGES), vsc_rows[r]
             )
-        nc.sync.dma_start(tok_rows[0:POOL_PAGES, :], vs[0].rearrange("(u c) -> u c", u=POOL_PAGES))
         ks_rows = k_scales[0].bitcast(I32).rearrange("(g r) c -> r g c", r=SCALE_ROWS)
         for r in range(SCALE_ROWS):
             nc.sync.dma_start(ks_pool[r:P:QUADRANT, :], ks_rows[r])
-        q_raw = [sb([P, PACK, NQ], F32, "q_raw%d" % b) for b in range(B)]
+        nc.sync.dma_start(tok_rows[0:POOL_PAGES, :], vs[0].rearrange("(u c) -> u c", u=POOL_PAGES))
+        q_raw = sb([P, B, PACK, NQ], F32, "q_raw")
         q_rows = qT.rearrange("b (p t) q -> b p (t q)", t=PACK)
-        nc.sync.dma_start(q_raw[0][:].rearrange("p t q -> p (t q)"), q_rows[0])
+        nc.sync.dma_start(q_raw[:, 0].rearrange("p t q -> p (t q)"), q_rows[0])
         kw_pool = sb([P, T], I32, "kw_pool")
         nc.sync.dma_start(kw_pool[:], k_words[0].rearrange("p n t -> p (n t)").bitcast(I32))
-        nc.sync.dma_start(q_raw[1][:].rearrange("p t q -> p (t q)"), q_rows[1])
+        nc.sync.dma_start(q_raw[:, 1].rearrange("p t q -> p (t q)"), q_rows[1])
 
+        nc.scalar.copy(
+            tok_pages[:, ZEROED_PAGES:, PACK:],
+            tok_rows[:, PACK:].unsqueeze(1).to_broadcast([P, POOL_PAGES - ZEROED_PAGES, PAGE - PACK]),
+        )
         bank = turn.tile([P, PACK, P], F32, name="bank", tag="turn")
         for t in range(PACK):
             nc.tensor.transpose(bank[:, t, :], tok_rows[:, t::PACK], ident[:])
         by_page = bank[:, :, 0:POOL_PAGES].rearrange("p t u -> p u t")
-        nc.scalar.copy(tok_pages[:, 0:ZEROED_PAGES, 0:PACK], by_page[:, 0:ZEROED_PAGES])
-        nc.scalar.copy(
-            tok_pages[:, ZEROED_PAGES:].rearrange("p u (c t) -> p u c t", t=PACK),
-            by_page[:, ZEROED_PAGES:].unsqueeze(2).to_broadcast([P, POOL_PAGES - ZEROED_PAGES, P, PACK]),
-        )
+        nc.scalar.copy(tok_pages[:, :, 0:PACK], by_page)
         q_bf = [sb([P, NQ, PACK], BF16, "q_bf%d" % b) for b in range(B)]
         for b in range(B):
             nc.scalar.copy(
-                q_bf[b][:].rearrange("p (c i) t -> p c t i", i=PACK), q_raw[b][:].rearrange("p t (c i) -> p c t i", i=PACK)
+                q_bf[b][:].rearrange("p (c i) t -> p c t i", i=PACK), q_raw[:, b].rearrange("p t (c i) -> p c t i", i=PACK)
             )
         vw_pool = sb([P, POOL_PAGES * DV], I32, "vw_pool")
         nc.sync.dma_start(
@@ -123,7 +124,7 @@ def tile_attend_pkv8_sigm_cap_kernel(tc, qT, k_words, k_scales, v_words, v_scale
         nc.vector.tensor_copy(vsc[:], vsc_pool[:].bitcast(U8).indirect(vlst[:]))
         nc.vector.tensor_copy(ks[:], ks_pool[:].bitcast(U8).indirect(lst[:]))
         early = EARLY_TOK_PAGES * PAGE
-        tok = sb([P, early], F32, "tok", "q_raw0")
+        tok = sb([P, early], F32, "tok")
         nc.vector.tensor_copy(tok[:], tok_pool[:].indirect(entries(lst, 0, early)))
         quantise_queries(0)
 
@@ -175,7 +176,7 @@ def tile_attend_pkv8_sigm_cap_kernel(tc, qT, k_words, k_scales, v_words, v_scale
             for page in range(b * SEQ_PAGES, (b + 1) * SEQ_PAGES):
                 finish(page)
 
-        tok_late = sb([P, B * N - early], F32, "tok_late", "q_raw1")
+        tok_late = sb([P, B * N - early], F32, "tok_late", "q_raw")
         nc.vector.tensor_copy(tok_late[:], tok_pool[:].indirect(entries(lst, early, B * N)))
         vw = sb([P, PAGES * DV], U32, "vw")
         nc.vector.tensor_copy(vw[:], vw_pool[:].bitcast(U32).indirect(vlst[:]))

from contextlib import ExitStack

import concourse.mybir as mybir
from concourse.masks import make_identity

F32 = mybir.dt.float32
BF16 = mybir.dt.bfloat16
I32 = mybir.dt.int32
U32 = mybir.dt.uint32
U16 = mybir.dt.uint16
U8 = mybir.dt.uint8
FP8X4 = mybir.dt.float8_e4m3fn_x4
ACT = mybir.ActivationFunctionType
ALU = mybir.AluOpType

P = 128
B, N, T, D, DV, NQ = 2, 1024, 4096, 512, 256, 128
PACK = 4
PAGE = P * PACK
SEQ_PAGES = N // PAGE
PAGES = B * SEQ_PAGES
POOL_PAGES = T // PAGE
LIST_ROWS = 16
QUADRANTS, QUADRANT, SCALE_ROWS = 4, 32, 4
VALUE_SCALE_ROW = 4
EARLY_TOK_PAGES = 3
ZEROED_PAGES = 4
CODE_BYTES = 4 * NQ
OUTER_AT = (16 * CODE_BYTES, 0)

FLOPS = 2 * B * NQ * N * (D + DV)
BYTES = 4 * B * D * NQ + (T * D + T * DV) * 33 // 32 + 4 * T + 2 * P * (B * N + PAGES * DV) // LIST_ROWS + 4 * B * NQ * DV


def tile_attend_pkv8_sigm_cap_kernel(tc, qT, k_words, k_scales, v_words, v_scales, vs, offs, voffs, out):
    nc = tc.nc
    with ExitStack() as ctx:
        keep = ctx.enter_context(tc.tile_pool(name="keep", bufs=1))
        shared = ctx.enter_context(tc.tile_pool(name="shared", bufs=1))
        turn = ctx.enter_context(tc.psum_pool(name="turn", bufs=PAGES))
        score = ctx.enter_context(tc.psum_pool(name="score", bufs=1))

        def sb(shape, dtype, name, tag=None):
            return keep.tile(shape, dtype, name=name, tag=tag or name, align_bytes=64)

        def placed(shape, dtype, name, offset):
            return shared.tile(shape, dtype, name=name, align_bytes=64, offset=offset)

        def entries(listing, first, last):
            return listing[:, first // LIST_ROWS : last // LIST_ROWS]

        lst = keep.tile([P, B * N // LIST_ROWS], U16, name="lst")
        vlst = keep.tile([P, PAGES * DV // LIST_ROWS], U16, name="vlst")
        ks_pool = sb([P, T // PACK], I32, "ks_pool")
        vsc_pool = sb([P, POOL_PAGES * DV // PACK], I32, "vsc_pool")
        tok_pool = sb([P, T], F32, "tok_pool")
        tok_pages = tok_pool[:].rearrange("p (u c) -> p u c", u=POOL_PAGES)

        ones = [sb([P, 1], F32, "one_" + tag, tag) for tag in ("q_raw", "kw_pool", "ident")]
        zero = sb([P, 1], F32, "zero")
        half = sb([P, 1], F32, "half")
        minus_two = sb([P, 1], F32, "minus_two")
        tok_rows = sb([P, PAGE], F32, "tok_rows", "vw_pool")
        nc.vector.memset(vsc_pool[:], 0)
        nc.vector.memset(ks_pool[:], 0)
        nc.vector.memset(tok_rows[:].bitcast(I32), 0)
        for one in ones:
            nc.vector.memset(one[:], 1.0)
        nc.vector.tensor_scalar(zero[:], ones[0][:], ones[1][:], ones[2][:], ALU.subtract, ALU.mult)
        ident = sb([P, P], F32, "ident")
        make_identity(nc, ident[:])
        nc.scalar.activation(half[:], zero[:], ACT.Sigmoid)
        nc.scalar.activation(minus_two[:], half[:], ACT.Copy, scale=-4.0)
        for first in range(0, ZEROED_PAGES, 2):
            nc.vector.memset(tok_pages[:, first : first + 2].bitcast(I32), 0)

        nc.sync.dma_start(vlst[:], voffs)
        nc.sync.dma_start(lst[:], offs)
        vsc_rows = v_scales.bitcast(I32).rearrange("u (g r) e -> r g u e", r=SCALE_ROWS)
        for r in range(SCALE_ROWS):
            nc.sync.dma_start(
                vsc_pool[VALUE_SCALE_ROW + r : P : QUADRANT, :].rearrange("g (u e) -> g u e", u=POOL_PAGES), vsc_rows[r]
            )
        ks_rows = k_scales[0].bitcast(I32).rearrange("(g r) c -> r g c", r=SCALE_ROWS)
        for r in range(SCALE_ROWS):
            nc.sync.dma_start(ks_pool[r:P:QUADRANT, :], ks_rows[r])
        nc.sync.dma_start(tok_rows[0:POOL_PAGES, :], vs[0].rearrange("(u c) -> u c", u=POOL_PAGES))
        q_raw = sb([P, B, PACK, NQ], F32, "q_raw")
        q_rows = qT.rearrange("b (p t) q -> b p (t q)", t=PACK)
        nc.sync.dma_start(q_raw[:, 0].rearrange("p t q -> p (t q)"), q_rows[0])
        kw_pool = sb([P, T], I32, "kw_pool")
        nc.sync.dma_start(kw_pool[:], k_words[0].rearrange("p n t -> p (n t)").bitcast(I32))
        nc.sync.dma_start(q_raw[:, 1].rearrange("p t q -> p (t q)"), q_rows[1])

        nc.scalar.copy(
            tok_pages[:, ZEROED_PAGES:, PACK:],
            tok_rows[:, PACK:].unsqueeze(1).to_broadcast([P, POOL_PAGES - ZEROED_PAGES, PAGE - PACK]),
        )
        bank = turn.tile([P, PACK, P], F32, name="bank", tag="turn")
        for t in range(PACK):
            nc.tensor.transpose(bank[:, t, :], tok_rows[:, t::PACK], ident[:])
        by_page = bank[:, :, 0:POOL_PAGES].rearrange("p t u -> p u t")
        nc.scalar.copy(tok_pages[:, :, 0:PACK], by_page)
        q_bf = [sb([P, NQ, PACK], BF16, "q_bf%d" % b) for b in range(B)]
        for b in range(B):
            nc.scalar.copy(
                q_bf[b][:].rearrange("p (c i) t -> p c t i", i=PACK), q_raw[:, b].rearrange("p t (c i) -> p c t i", i=PACK)
            )
        vw_pool = sb([P, POOL_PAGES * DV], I32, "vw_pool")
        nc.sync.dma_start(
            vw_pool[:].rearrange("p (u e) -> p u e", u=POOL_PAGES),
            v_words.rearrange("u p e t -> p u (e t)").bitcast(I32),
        )

        ks = sb([P, B * N], U8, "ks")
        q_codes = sb([P, B * NQ], U32, "q_codes")
        q_sc = sb([P, B * NQ], U8, "q_sc")
        vsc = sb([P, PAGES * DV], U8, "vsc")

        def quantise_queries(b):
            cols = slice(b * NQ, (b + 1) * NQ)
            nc.vector.quantize_mx(q_codes[:, cols].bitcast(FP8X4), q_sc[:, cols], q_bf[b][:].rearrange("p q t -> p (q t)"))

        nc.vector.tensor_copy(vsc[:], vsc_pool[:].bitcast(U8).indirect(vlst[:]))
        nc.vector.tensor_copy(ks[:], ks_pool[:].bitcast(U8).indirect(lst[:]))
        early = EARLY_TOK_PAGES * PAGE
        tok = sb([P, early], F32, "tok")
        nc.vector.tensor_copy(tok[:], tok_pool[:].indirect(entries(lst, 0, early)))
        quantise_queries(0)

        kw = [sb([P, PAGE], U32, "kw%d" % page) for page in range(PAGES)]
        for page in range(PAGES):
            tokens = entries(lst, page * PAGE, (page + 1) * PAGE)
            nc.vector.tensor_copy(kw[page][:], kw_pool[:].bitcast(U32).indirect(tokens))
        quantise_queries(1)
        inner = [sb([P, PACK, P], F32, "inner%d" % page) for page in range(PAGES)]
        prob = [None] * PAGES

        def inner_sigmoid(page):
            queries = slice(page // SEQ_PAGES * NQ, (page // SEQ_PAGES + 1) * NQ)
            sc = score.tile([P, PAGE], F32, name="sc%d" % page)
            nc.tensor.matmul_mx(
                sc[:],
                lhsT=q_codes[:, queries].bitcast(FP8X4),
                lhsT_scale=q_sc[:, queries],
                rhs=kw[page][:].bitcast(FP8X4),
                rhs_scale=ks[:, page * PAGE : (page + 1) * PAGE],
                start=True,
                stop=True,
            )
            nc.scalar.activation(
                inner[page][:].rearrange("p t (c i) -> p c t i", i=PACK),
                sc[:].rearrange("p (c i t) -> p c t i", i=PACK, t=PACK),
                ACT.Sigmoid,
            )

        def turned(dealt):
            bank = turn.tile([P, PACK, NQ], F32, name="bank", tag="turn")
            for t in range(PACK):
                nc.tensor.transpose(bank[:, t, :], dealt[:, t, :], ident[:])
            return bank[:].rearrange("p t q -> p q t")

        def outer_then_turn(page):
            outer = placed([P, PACK, P], F32, "outer%d" % page, OUTER_AT[page])
            nc.scalar.activation(outer[:], inner[page][:], ACT.Sigmoid, scale=4.0, bias=minus_two[:])
            prob[page] = turned(outer)

        def turn_then_outer(page):
            outer = sb([P, NQ, PACK], F32, "outer%d" % page)
            nc.scalar.activation(outer[:], turned(inner[page]), ACT.Sigmoid, scale=4.0, bias=minus_two[:])
            prob[page] = outer[:]

        for b, finish in enumerate((outer_then_turn, turn_then_outer)):
            for page in range(b * SEQ_PAGES, (b + 1) * SEQ_PAGES):
                inner_sigmoid(page)
            for page in range(b * SEQ_PAGES, (b + 1) * SEQ_PAGES):
                finish(page)

        tok_late = sb([P, B * N - early], F32, "tok_late", "q_raw")
        nc.vector.tensor_copy(tok_late[:], tok_pool[:].indirect(entries(lst, early, B * N)))
        vw = sb([P, PAGES * DV], U32, "vw")
        nc.vector.tensor_copy(vw[:], vw_pool[:].bitcast(U32).indirect(vlst[:]))

        w_all = sb([P, PAGES, NQ, PACK], BF16, "w_bf", "vw_pool")
        w_bf = [w_all[:, page] for page in range(PAGES)]
        w_codes = [
            placed([P, NQ], U32, "w_codes0", 0),
            sb([P, NQ], U32, "w_codes1"),
            sb([P, NQ], U32, "w_codes2", "minus_two"),
            sb([P, NQ], U32, "w_codes3"),
        ]
        w_sc = sb([P, PAGES * NQ], U8, "w_sc")
        y = [score.tile([P, DV], F32, name="y%d" % b, tag="sc%d" % (PAGES - 1 - b)) for b in range(B)]

        def product(page):
            held, first = (tok, 0) if page < EARLY_TOK_PAGES else (tok_late, EARLY_TOK_PAGES)
            scales = held[:, (page - first) * PAGE : (page - first) * PAGE + PACK].unsqueeze(1).to_broadcast([P, NQ, PACK])
            nc.vector.tensor_tensor(w_bf[page], prob[page], scales, ALU.mult)

        def weigh_values(page):
            cols = slice(page * NQ, (page + 1) * NQ)
            nc.vector.quantize_mx(
                w_codes[page][:].bitcast(FP8X4), w_sc[:, cols], w_bf[page].rearrange("p q t -> p (q t)")
            )
            b, nth = divmod(page, SEQ_PAGES)
            nc.tensor.matmul_mx(
                y[b][:],
                lhsT=w_codes[page][:].bitcast(FP8X4),
                lhsT_scale=w_sc[:, cols],
                rhs=vw[:, page * DV : (page + 1) * DV].bitcast(FP8X4),
                rhs_scale=vsc[VALUE_SCALE_ROW:P, page * DV : (page + 1) * DV],
                start=(nth == 0),
                stop=(nth == SEQ_PAGES - 1),
            )
            if nth == SEQ_PAGES - 1:
                res = sb([P, DV], F32, "res%d" % b)
                nc.scalar.activation(res[:], y[b][:], ACT.Copy, scale=1.0 / 16.0)
                nc.sync.dma_start(out[b], res[:])

        product(0)
        product(1)
        weigh_values(0)
        product(2)
        weigh_values(1)
        product(3)
        weigh_values(2)
        weigh_values(3)
